import numpy as np, ml_dtypes
CORES = [10,34,74,98]
N = 4
BF = ml_dtypes.bfloat16
def gentries(a):
    return np.ascontiguousarray(a.reshape(8, 16, -1).transpose(0, 2, 1)).reshape(8, -1)
def gtable(e):
    e = np.asarray(e); return np.ascontiguousarray(e.reshape(8, -1, 16).transpose(0, 2, 1)).reshape(128, -1).astype(np.int32)
V, H, K, Q, PO, HP = 2048, 1024, 4, 512, 4, 3
W = V + 2 * H
ALL = (N, 8, 16, V)
def bases(rng):
    return rng.integers(32, 65, (1, 1, 16, 1)) * (1 - 2 * rng.integers(0, 2, (1, 1, 16, 1)))
def sky(rng, base, c):
    main = rng.choice(np.array([0, 1, 2]), (N, 8, 1, V), p=np.array([0.45, 0.35, 0.2]))
    camp = np.where(rng.random(ALL) < 0.3, rng.integers(0, 3, ALL), main)
    t = base + np.array([-90, 0, 90])[camp] + np.rint(c * rng.integers(-40, 41, ALL)).astype(np.int64)
    d = np.clip(np.rint(c * rng.integers(32, 129, ALL)), 32, 128).astype(np.int64)
    return t, d, drifts(rng)
def drifts(rng):
    return rng.integers(-256, 257, ALL) * np.where(rng.random((N, 8, 1, V)) < 0.5, 4, 1)
def agree(rng, base, ms):
    m = rng.choice(np.array(ms), (N, 8, 1, V)); off = np.argsort(rng.random(ALL), axis=2) >= m
    far = rng.integers(150, 181, ALL) * (1 - 2 * rng.integers(0, 2, ALL))
    return base + rng.integers(-8, 9, ALL) + np.where(off, far, 0), rng.integers(112, 129, ALL)
def nets(rng):
    o = np.argsort(rng.random((N, 8, V)), axis=-1); place = np.argsort(o, axis=-1)
    mate = np.take_along_axis(o[:, :, None], ((place >> 3) << 3)[:, :, None] + rng.integers(0, 8, (N, 8, K, V)), 3)
    u = rng.random((N, 8, K, V))
    s = np.where(u < 0.55, mate, np.where(u < 0.75, rng.integers(0, V, u.shape), rng.integers(V, W, u.shape)))
    j = rng.integers(0, K, (N, 8, 1, V))
    r = np.where(rng.random((N, 8, V)) < 0.8, np.take_along_axis(s, j, 2)[:, :, 0], rng.integers(0, W, (N, 8, V)))
    return s, r
def ring(rng):
    n = rng.integers(1, HP + 4, V); last = np.add.accumulate(n); i = np.arange(V)
    c = np.searchsorted(last, i, side="right"); first = last[c] - n[c]
    nx = np.where(i + 1 < np.minimum(last[c], V), i + 1, first); o = rng.permutation(V)
    y = np.zeros(V, np.int64); y[o] = o[nx]
    return y
def pack(t, d, f, s, r):
    e = np.ascontiguousarray(s.reshape(N, 8, K, 4, Q).transpose(0, 1, 3, 2, 4)).reshape(N, 8, K * V)
    return {"th": (t * 0.015625).astype(np.float32).astype(BF).reshape(N, 128, V), "dl": (d * 0.0078125).astype(np.float32).astype(BF).reshape(N, 128, V),
            "dr": (f * 0.0000152587890625).astype(np.float32).astype(BF).reshape(N, 128, V), "sl": np.stack([gtable(a) for a in e]), "rf": np.stack([gtable(a) for a in r])}
def setup_inputs(rng):
    t, d, f = sky(rng, bases(rng), 1.0); s, r = nets(rng)
    return pack(t, d, f, s, r)
def setup_inputs_corners(rng):
    base = bases(rng); t, d = agree(rng, base, [16, 16, 16, 15, 9, 9, 8, 8, 1, 0]); tc, dc = agree(rng, base, [16]); f = drifts(rng); s, r = nets(rng)
    calm = ((np.arange(N)[:, None] + np.arange(8)) & 1) == 0
    t = np.where(calm[:, :, None, None], tc, t); d = np.where(calm[:, :, None, None], dc, d)
    pts = np.array([0, V - 1, V, V + H - 1, V + H, W - 1])
    s = np.where(rng.random(s.shape) < 0.2, rng.choice(pts, s.shape), s); u = rng.random(r.shape)
    r = np.where(u < 0.5, rng.choice(pts, r.shape), np.where(u < 0.65, np.arange(V), r))
    for q in range(N):
        for g in range(8):
            if calm[q, g]:
                y = ring(rng); s[q, g, 0] = y; r[q, g] = y
    return pack(t, d, f, s, r)
def setup_inputs_crowd(rng):
    base = bases(rng); t, d, f = sky(rng, base, 1.0); s, r = nets(rng); tc, dc = agree(rng, base, [16, 15])
    kind = (np.arange(N)[:, None] + np.arange(8) + rng.integers(0, 4)) & 3; k = kind[:, :, None, None]
    t = np.where(k < 3, tc, t); d = np.where(k < 3, dc, d)
    one = rng.integers(0, W, (N, 8, 1, 1)); one[N - 1] = V - 1; one[:, 7] = W - 1
    few = rng.integers(0, W, (N, 8, 3)); three = np.take_along_axis(few, rng.integers(0, 3, (N, 8, K * V)), 2).reshape(N, 8, K, V)
    spare = np.arange(K)[:, None] == rng.integers(0, K, (N, 8, 1, V))
    s = np.where(k == 0, one, np.where(k == 1, np.where(spare, s, one), np.where(k == 2, three, s)))
    r = np.where(kind[:, :, None] < 2, one[:, :, 0], r)
    return pack(t, d, f, s, r)
def setup_inputs_ends(rng):
    t, d, f = sky(rng, bases(rng), 1.0); s, r = nets(rng); one = (N, 8, 1, V)
    flip = np.where(rng.random(ALL) < 0.25, -1, 1)
    t = np.where(rng.random(one) < 0.8, 256 * (1 - 2 * rng.integers(0, 2, one)) * flip, t)
    d = np.where(rng.random(one) < 0.8, rng.choice(np.array([32, 128]), ALL), d)
    f = np.where(rng.random(one) < 0.8, 1024 * (1 - 2 * rng.integers(0, 2, ALL)), f)
    s = np.where(rng.random(s.shape) < 0.7, rng.choice(np.array([0, W - 1]), s.shape), s)
    r = np.where(rng.random(r.shape) < 0.7, rng.choice(np.array([0, W - 1]), r.shape), r)
    v = np.arange(V); ix = v[(v % Q < 4) | (v % Q >= Q - 4)]; odd = (ix & 1) == 1; n = (N, 8, len(ix))
    t[..., ix] = np.where(odd, -256, 256); d[..., ix] = 128; f[..., ix] = np.where((ix & 2) == 2, -1024, 1024)
    for j in range(K):
        a, b = rng.choice(ix[odd], n), rng.choice(ix[~odd], n)
        s[:, :, j, ix] = np.where(odd, a, b) if j < K - 1 else np.where(odd, b, a)
    return pack(t, d, f, s, r)
def setup_inputs_spread(rng):
    c = np.exp2(rng.integers(-1, 2, (N, 8, 1, V)).astype(np.float64)); t, d, f = sky(rng, bases(rng), c); s, r = nets(rng)
    f = rng.integers(-256, 257, ALL) * (1 << rng.integers(0, 3, (N, 8, 1, V)))
    s = np.where(rng.random((N, 8, 1, V)) < 0.4, (W * rng.random(s.shape) ** 3).astype(np.int64), s)
    return pack(t, d, f, s, r)
def setup_inputs_ties(rng):
    base = rng.choice(np.array([-64, -32, 32, 64]), (1, 1, 16, 1)); s, r = nets(rng)
    main = rng.integers(-3, 4, (N, 8, 1, V)); t = base + 32 * np.where(rng.random(ALL) < 0.3, rng.integers(-3, 4, ALL), main)
    d = rng.choice(np.array([32, 64, 128]), ALL)
    f = rng.choice(np.array([0, 0, 0, 0, 0, 0, 0, 1, -1, 1024, -1024]), (N, 8, 1, V)) * rng.integers(0, 2, ALL)
    return pack(t, d, f, s, r)
def check_ranges(d):
    bad = []
    for k, lo, hi, u in (("th", -4.0, 4.0, 64.0), ("dl", 0.25, 1.0, 128.0), ("dr", -0.015625, 0.015625, 65536.0)):
        v = np.asarray(d[k]).astype(np.float64)
        if not (np.min(v) >= lo and np.max(v) <= hi): bad.append("range of " + k)
        elif np.any(np.rint(v * u) != v * u): bad.append("multiples of " + k)
    for k in ("sl", "rf"):
        if np.min(d[k]) < 0 or np.max(d[k]) > W - 1: bad.append("range of " + k)
    return bad
def view(a):
    return np.concatenate([a, np.roll(a, -1, axis=0)[..., :H], np.roll(a, -1, axis=1)[..., :H]], axis=3)
def reference(th, dl, dr, sl, rf):
    x, e, f = [a.astype(np.float64).reshape(N, 8, 16, V) for a in (th, dl, dr)]
    S = np.stack([gentries(a) for a in sl]).astype(np.int64).reshape(N, 8, 4, K, Q).transpose(0, 1, 3, 2, 4).reshape(N, 8, K, V)
    R = np.stack([gentries(a) for a in rf]).astype(np.int64)
    away = np.broadcast_to(np.arange(V, W), (N, 8, 2 * H))
    for poll in range(PO):
        ids = np.concatenate([np.arange(Q) + (poll & 1) * Q, np.arange(Q) + (2 + (poll & 1)) * Q])
        xw, ew, Sw = view(x), view(e), view(S); Sp = S[..., ids]; xo, eo = x[..., ids], e[..., ids]
        lo, hi = [], []
        for j in range(K):
            ix = Sp[:, :, j][:, :, None, :]; a = np.take_along_axis(xw, ix, 3); b = np.take_along_axis(ew, ix, 3)
            lo.append(a - b); hi.append(a + b)
        lo.append(xo - eo); hi.append(xo + eo)
        cnt = []
        for a in lo:
            c = np.zeros(a.shape, np.int64)
            for b, h in zip(lo, hi): c += (b <= a) & (a <= h)
            cnt.append(c)
        best = np.maximum.reduce(cnt)
        A = np.maximum.reduce([np.where(c == best, a, -64.0) for c, a in zip(cnt, lo)])
        hold = [(b <= A) & (A <= h) for b, h in zip(lo, hi)]
        B = np.minimum.reduce([np.where(m, h, 64.0) for m, h in zip(hold, hi)])
        n = np.stack([np.add.reduce(m.astype(np.int64), axis=2) for m in hold[:K]], axis=2)
        stay = n >= 9; score = np.where(stay, n, 0); top = np.argmax(score, axis=2); some = np.max(score, axis=2) > 0
        cand = np.take_along_axis(Sp, top[:, :, None], 2)[:, :, 0]
        Rw = np.concatenate([R, away], axis=2); h = cand; meet = h == ids
        for hop in range(HP):
            h = np.take_along_axis(Rw, h, 2); meet = meet | (h == ids)
        veto = some & meet
        fall = ~stay | (veto[:, :, None] & (np.arange(K)[:, None] == top[:, :, None]))
        w = np.where(some & ~meet, cand, R[..., ids]); ww = w[:, :, None]
        nm = np.take_along_axis(Sw, ww, 3)
        new = np.where(ww < V, nm, np.where(ww < V + H, V, V + H) + nm)
        Sn = np.where(fall & ((ww < V) | (nm < H)), new, Sp)
        x = x + f; e = e + 0.0625
        x[..., ids] = A + 0.5 * (B - A); e[..., ids] = 0.5 * (B - A) + 0.0625
        S = np.array(S); S[..., ids] = Sn; R = np.array(R); R[..., ids] = w
    xw, ew = view(x), view(e); y = 0.5 * e
    for j in range(K):
        ix = S[:, :, j][:, :, None, :]; z = np.take_along_axis(xw, ix, 3) - x
        y = y + np.take_along_axis(ew, ix, 3) * np.reciprocal(1.0 + np.exp(-z))
    return {"yt": x.reshape(N, 128, V).astype(np.float32), "yq": y.reshape(N, 128, V).astype(np.float32), "yr": np.asarray(R, np.float32)}

def check_inputs(d):
    bad = list(check_ranges(d))
    if not bad:
        for name, y in reference(**d).items():
            for q in range(N):
                v = np.abs(np.asarray(y[q], np.float64)); s = np.sqrt(np.mean(v * v))
                if v.max() > 11 * s or s < 2.0 ** -2: bad.append('%s of rank %d is uneven or too small' % (name, q))
    return bad

@@ -1,0 +1,726 @@
+from concourse.bass import DstId, RemoteDMATransfer
+from concourse.mybir import AluOpType, ActivationFunctionType
+
+F, B, I, U = "float32", "bfloat16", "int32", "uint16"
+NG, NS, NR = 30, 68, 24
+SCRATCH = {
+    "LO0": ("sbuf", [128, 4096], F), "LO1": ("sbuf", [128, 4096], F),
+    "HI0": ("sbuf", [128, 4096], F), "HI1": ("sbuf", [128, 4096], F),
+    "ST": ("sbuf", [128, 4096], B), "RT": ("sbuf", [128, 2064], B),
+    "FM": ("sbuf", [128, 2048], F), "FS": ("sbuf", [128, 2048], B), "AS": ("sbuf", [128, 256], F),
+    "TMP": ("sbuf", [128, 1024], F), "ZM": ("sbuf", [128, 2304], B),
+    "SLI": ("sbuf", [128, 4, 4, 32], I), "RFI": ("sbuf", [128, 2, 2, 32], I), "RF": ("sbuf", [128, 2, 2, 32], F),
+    "RFT": ("sbuf", [128, 128], F), "SG": ("sbuf", [128, 64, 16], B),
+    "XI": ("sbuf", [128, 144], F), "XD": ("sbuf", [128, 128], F),
+    "IDB": ("sbuf", [128, 128], B), "IDN": ("sbuf", [128, 128], B), "IDF": ("sbuf", [128, 128], F),
+    "IDH": ("sbuf", [128, 128], F),
+    "UP": ("sbuf", [128, 288], B), "UN": ("sbuf", [128, 288], B), "YM": ("sbuf", [128, 720], B),
+    "PC": ("sbuf", [128, 8], I), "PF": ("sbuf", [128, 32], F),
+    "VC0": ("sbuf", [128, 4, 2, 32], F), "VC1": ("sbuf", [128, 4, 2, 32], F), "CJ": ("sbuf", [128, 64], B),
+    "KS0": ("sbuf", [128, 4, 2, 32], F), "KS1": ("sbuf", [128, 4, 2, 32], F), "M2": ("sbuf", [128, 128], F), "KT": ("sbuf", [128, 64], I),
+    "CA": ("sbuf", [128, 64], I), "IX": ("sbuf", [128, 256], U), "SM": ("sbuf", [128, 640], F),
+    "EQ": ("sbuf", [128, 256], F), "STAY": ("sbuf", [128, 256], F), "OK": ("sbuf", [128, 256], F),
+    "DH": ("sbuf", [128, 320], B), "DL": ("sbuf", [128, 320], B), "GB": ("sbuf", [128, 1024], B),
+    "KA": ("psum", [128, 1536], F), "KB": ("psum", [128, 1536], F),
+    "PL": ("psum", [128, 512], F), "PI": ("psum", [128, 512], F),
+}
+for _k in range(4):
+    SCRATCH["GL%d" % _k] = ("sbuf", [128, 1280], F)
+    SCRATCH["GH%d" % _k] = ("sbuf", [128, 1280], F)
+for _k in range(2):
+    SCRATCH["IN%d" % _k] = ("sbuf", [128, 7680], B)
+    SCRATCH["LE%d" % _k] = ("sbuf", [128, 1024], B)
+    SCRATCH["LT%d" % _k] = ("sbuf", [128, 1280], B)
+    SCRATCH["KC%d" % _k] = ("sbuf", [128, 512], F)
+    SCRATCH["RB%d" % _k] = ("sbuf", [128, 256], F)
+    SCRATCH["ZB%d" % _k] = ("sbuf", [128, 256], F)
+    SCRATCH["NA%d" % _k] = ("sbuf", [128, 1280], F)
+    SCRATCH["SP%d" % _k] = ("sbuf", [128, 5, 2, 32], F)
+    SCRATCH["SU%d" % _k] = ("sbuf", [128, 256], U)
+    SCRATCH["YB%d" % _k] = ("sbuf", [128, 512], F)
+SEMAPHORES = (["e_pe", "e_dve", "e_act", "e_pool"] + ["dg%d" % k for k in range(NG)] + ["ds%d" % k for k in range(NS)]
+              + ["rl%d" % k for k in range(NR)] + ["rr%d" % k for k in range(NR)])
+
+CY, PCY, GA, HOP = 1.0, 0.5, 1.56, 120.0
+THR = 9 * 16384
+RND1 = 1.5 * 2.0 ** 23
+RND64 = 1.5 * 2.0 ** 29
+SIZE = {F: 4, I: 4, B: 2, U: 2}
+LAST = {}
+OPT = {"boost": 3000.0, "ract": True, "g0": 3, "fin": (2, 2, 2, 2), "look": 50.0, "tail": (0.0, 0.0, 0.0, 0.0),
+       "nadma": False, "cuts": (0, 2, 5), "short": (1, 3), "turns": 6, "mix": 0.5,
+       "ds": 1.2, "rs": 1.0, "ps": 1.0, "gs": 1.1,
+       "split": (0, 3), "sep": True, "pe0": True, "presum": False}
+
+
+def build(g, core, T, topo):
+    A = AluOpType
+    AF = ActivationFunctionType
+    n = len(T.cores)
+    rank = T.rank_of(core)
+    down, up = T.cores[(rank - 1) % n], T.cores[(rank + 1) % n]
+    ops = []
+    hist = {}
+    boost = [0.0]
+
+    def ap(name, *idx):
+        shape = list(T[name].shape)
+        idx = list(idx) + [slice(None)] * (len(shape) - len(idx))
+        lo, hi, cnt, stride, pr = 0, 0, 1, 1, None
+        for d in range(len(shape) - 1, -1, -1):
+            x = idx[d]
+            r = range(x, x + 1) if isinstance(x, int) else range(*x.indices(shape[d]))
+            if d == 0:
+                pr = (r[0], r[-1] + 1)
+            else:
+                lo += r[0] * stride
+                hi += r[-1] * stride
+                cnt *= len(r)
+                stride *= shape[d]
+        where, dtype = (SCRATCH[name][0], SCRATCH[name][2]) if name in SCRATCH else ("dram", F)
+        return {"a": T[name][tuple(idx)], "n": name, "p": pr, "lo": lo, "hi": hi + 1, "cnt": cnt,
+                "ps": where == "psum", "sz": SIZE[dtype]}
+
+    def c2(name, a, b, step=1):
+        return ap(name, slice(None), slice(a, b, step))
+
+    def add(eng, kind, emit, R, W, dur, lat=0.0):
+        me = len(ops)
+        deps = set()
+        for acc, wr in [(x, False) for x in R] + [(x, True) for x in W]:
+            for e in hist.get(acc["n"], []):
+                if e[0] < acc["hi"] and acc["lo"] < e[1] and e[2] < acc["p"][1] and acc["p"][0] < e[3] and e[4] != me:
+                    if e[5]:
+                        deps.add((e[4], "W"))
+                    elif wr:
+                        deps.add((e[4], "R"))
+            h = hist.setdefault(acc["n"], [])
+            if wr:
+                h[:] = [e for e in h if not (acc["lo"] <= e[0] and e[1] <= acc["hi"] and acc["p"][0] <= e[2]
+                                             and e[3] <= acc["p"][1] and acc.get("full", True))]
+            h.append((acc["lo"], acc["hi"], acc["p"][0], acc["p"][1], me, wr))
+        banks = set()
+        for acc in R + W:
+            if acc["ps"]:
+                for b in range(acc["lo"] // 512, (acc["hi"] - 1) // 512 + 1):
+                    banks.add((acc["n"], b))
+        ops.append({"eng": eng, "kind": kind, "emit": emit, "deps": deps, "dur": dur, "lat": lat, "banks": banks,
+                    "tag": "%s:%d" % (W[0]["n"], W[0]["lo"]), "boost": boost[0]})
+        return me
+
+    def part(x):
+        if x["cnt"] != x["hi"] - x["lo"]:
+            x = dict(x)
+            x["full"] = False
+        return x
+
+    def tt(out, a, b, op, win=None):
+        cyc = 1 if (a["ps"] or b["ps"]) else 2
+        add("dve", "c", lambda e: [e.tensor_tensor(out["a"], a["a"], b["a"], op)], [a, b], [part(out)],
+            50 + max(64, out["cnt"] * cyc) * CY)
+
+    def ts(out, a, s1, s2, op0, op1=None):
+        R = [a] + [s for s in (s1, s2) if isinstance(s, dict)]
+        v1 = s1["a"] if isinstance(s1, dict) else s1
+        v2 = s2["a"] if isinstance(s2, dict) else s2
+        half = 0.5 if out["sz"] == 2 and a["sz"] == 2 else 1
+
+        def emit(e):
+            if op1 is None:
+                return [e.tensor_scalar(out["a"], a["a"], v1, None, op0)]
+            return [e.tensor_scalar(out["a"], a["a"], v1, v2, op0, op1)]
+        add("dve", "c", emit, R, [part(out)], 50 + max(64, out["cnt"] * half) * CY)
+
+    def cp(out, a):
+        add("dve", "c", lambda e: [e.tensor_copy(out["a"], a["a"])], [a], [part(out)], 50 + max(64, out["cnt"]) * CY)
+
+    def act(out, a, scale=1.0, bias=0.0, func=None):
+        f = func if func is not None else (AF.Copy if bias == 0.0 else AF.Identity)
+        add("act", "c", lambda e: [e.activation(out["a"], a["a"], f, bias=bias, scale=scale)], [a], [part(out)],
+            65 + max(64, out["cnt"]) * CY)
+
+    def acts(pairs):
+        add("act", "c", lambda e: [e.activation(o["a"], a["a"], AF.Copy) for o, a in pairs],
+            [a for o, a in pairs], [part(o) for o, a in pairs], sum(65 + max(64, o["cnt"]) * CY for o, a in pairs))
+
+    def gather(eng, out, win, off, scale=1.0, other=None, op=None):
+        dur = 60 + out["cnt"] * GA * CY
+        if eng == "act":
+            add("act", "c", lambda e: [e.activation(out["a"], win["a"].indirect(off["a"]), AF.Copy, scale=scale)],
+                [win, off], [out], dur)
+        elif other is None:
+            add("dve", "c", lambda e: [e.tensor_copy(out["a"], win["a"].indirect(off["a"]))], [win, off], [out], dur)
+        else:
+            add("dve", "c", lambda e: [e.tensor_tensor(out["a"], win["a"].indirect(off["a"]), other["a"], op)],
+                [win, off, other], [out], dur)
+        ops[-1]["gat"] = True
+
+    def mm(items):
+        R, W, dur = [], [], 0.0
+        for o, l, r, st, sp in items:
+            R += [l, r] + ([] if st else [o])
+            W.append(part(o))
+            dur += (max(64, r["cnt"]) * (4 if r["sz"] == 4 else 1) + 16) * PCY
+        add("pe", "c", lambda e: [e.matmul(o["a"], l["a"], r["a"], st, sp) for o, l, r, st, sp in items], R, W, dur, 60)
+
+    def iota(out, pattern, base, mult):
+        kw = {} if SCRATCH[out["n"]][2] == I else {"allow_small_or_imprecise_dtypes": True}
+        add("pool", "c", lambda e: [e.iota(out["a"], pattern, base, mult, **kw)], [], [out], 130 + 2 * out["cnt"] * CY)
+
+    def dma(out, a, accum=False):
+        side = out if out["n"] in SCRATCH else a
+        by = side["cnt"] * side["sz"] * (side["p"][1] - side["p"][0])
+        if accum:
+            add("pool", "d", lambda e: [e.dma_start(out["a"], a["a"], accum_op=A.add)], [a, out], [part(out)],
+                900.0, 1800 + by / 300.0)
+        else:
+            add("sync", "d", lambda e: [e.dma_start(out["a"], a["a"])], [a], [part(out)], 100.0, 1800 + by / 500.0)
+
+    nrem = [0]
+
+    def send(pairs):
+        k = nrem[0]
+        nrem[0] += 1
+        eng = topo.engines(core, down)
+        per = len(eng) // len(pairs)
+        rid, pid = topo.addr(down)[0], topo.addr(down)[1]
+
+        def emit(e):
+            tr = [RemoteDMATransfer(dst_ids=[DstId(rid=rid, pnc=pid)],
+                                    dma_engine_mask=sum(1 << x for x in eng[j * per:(j + 1) * per]),
+                                    remote_sem=T.sem["rr%d" % k], src=s["a"], dst=d["a"])
+                  for j, (d, s) in enumerate(pairs)]
+            e.remote_dma_fused(tr, local_sem=T.sem["rl%d" % k])
+        by = sum(s["cnt"] * s["sz"] * 128 for d, s in pairs)
+        me = add("pool", "r", emit, [s for d, s in pairs], [d for d, s in pairs], 1000.0, 2500 + by / 70.0)
+        ops[me]["rem"] = (k, per * len(pairs))
+
+    def credit(regions):
+        k = nrem[0]
+        nrem[0] += 1
+        rid, pid = topo.addr(up)[0], topo.addr(up)[1]
+        m = 1 << topo.engines(core, up)[0]
+        me = add("pool", "r", lambda e: e.remote_sem_update(T.sem["rr%d" % k], T.sem["rl%d" % k], pid, rid, m),
+                 [], regions, 800.0, 2500.0)
+        ops[me]["rem"] = (k, 1)
+
+    def shift(name, a, w):
+        dma(ap(name, slice(0, 112), slice(3072 + a, 3072 + a + w)), ap(name, slice(16, 128), slice(a, a + w)))
+        dma(ap(name, slice(112, 128), slice(3072 + a, 3072 + a + w)), ap(name, slice(0, 16), slice(a, a + w)))
+
+    def publish(names, a, w):
+        send([(c2(x, 2048 + a, 2048 + a + w), c2(x, a, a + w)) for x in names])
+        for x in names:
+            shift(x, a, w)
+
+    idb, idn, idf, idh = ap("IDB"), ap("IDN"), ap("IDF"), ap("IDH")
+
+    dma(c2("IN1", 0, 1024), c2("th", 0, 1024))
+    dma(c2("IN1", 1024, 2048), c2("dl", 0, 1024))
+    iota(ap("XD"), [[1, 128]], 0, -1)
+    send([(c2("IN1", 4096, 6144), c2("IN1", 0, 2048))])
+    dma(c2("IN1", 2048, 3072), c2("th", 1024, 2048))
+    dma(c2("IN1", 3072, 4096), c2("dl", 1024, 2048))
+    dma(ap("SLI"), ap("sl"))
+    dma(ap("RFI"), ap("rf"))
+    dma(ap("FS"), ap("dr"))
+    ts(idb, ap("XD"), 0.0, None, A.is_equal)
+    ts(idn, ap("XD"), 0.0, -1.0, A.is_equal, A.mult)
+    ts(idf, ap("XD"), 0.0, None, A.is_equal)
+    ts(idh, ap("XD"), 0.0, 0.5, A.is_equal, A.mult)
+    iota(c2("PC", 0, 1), [[0, 1]], 0, 1)
+    iota(ap("XI"), [[1, 144]], -16, 0)
+    iota(c2("OK", 0, 256), [[0, 4], [1024, 2], [16, 32]], 0, 0)
+    iota(ap("CJ"), [[-4096, 4], [0, 16]], 12288, 0)
+    ts(c2("PC", 1, 2), c2("PC", 0, 1), 112, None, A.bitwise_and)
+    ts(c2("PC", 2, 3), c2("PC", 0, 1), 15, None, A.bitwise_and)
+    ts(c2("PC", 3, 4), c2("PC", 2, 3), 1, None, A.arith_shift_right)
+    cp(c2("PF", 0, 4), c2("PC", 0, 4))
+    g16, pm, ph = c2("PF", 1, 2), c2("PF", 2, 3), c2("PF", 3, 4)
+    ts(c2("PF", 16, 32), c2("XI", 16, 32), pm, None, A.is_equal)
+    ts(c2("PF", 8, 16), c2("XI", 16, 24), ph, None, A.is_equal)
+    ts(c2("PF", 5, 6), pm, 8.0, 2048.0, A.is_equal, A.mult)
+    for a, w in ((0, 8192.0), (144, 16384.0)):
+        ts(c2("UP", a, a + 144), ap("XI"), g16, w, A.is_equal, A.mult)
+        ts(c2("UN", a, a + 144), ap("XI"), g16, -w, A.is_equal, A.mult)
+    for j in range(5):
+        ts(c2("YM", 144 * j, 144 * j + 144), ap("XI"), g16, c2("PF", 8 + j, 9 + j), A.is_equal, A.mult)
+    for r in range(16):
+        ts(c2("ZM", 144 * r, 144 * r + 144), ap("XI"), g16, c2("PF", 16 + r, 17 + r), A.is_equal, A.mult)
+    ts(ap("VC0"), ap("OK"), pm, None, A.add)
+    ts(ap("VC1"), ap("VC0"), 512.0, None, A.add)
+    ts(c2("RT", 2048, 2064), c2("XI", 0, 16), 0.0, c2("PF", 5, 6), A.mult, A.add)
+    for par in range(2):
+        for kk in range(2):
+            cp(ap("SP%d" % par, slice(None), slice(0, 4), kk), ap("SLI", slice(None), par + 2 * kk))
+        cp(ap("SP%d" % par, slice(None), 4), ap("RFI", slice(None), slice(None), par))
+        for kk in range(2):
+            cp(c2("SU%d" % par, 128 * kk, 128 * kk + 128), ap("SLI", slice(None), par + 2 * kk))
+
+    bank = [("KA", 0), ("KA", 512), ("KA", 1024), ("KB", 0), ("KB", 512), ("KB", 1024)]
+    nb = [0]
+
+    def ends(src, dst0):
+        for a in (0, 512):
+            for tab, sg in (("LO0", idn), ("HI0", idb)):
+                bn, bo = bank[nb[0] % 6]
+                nb[0] += 1
+                ps = c2(bn, bo, bo + 512)
+                mm([(ps, idb, c2("IN1", src + a, src + a + 512), True, False),
+                    (ps, sg, c2("IN1", src + 1024 + a, src + 1536 + a), False, True)])
+                if tab == "LO0":
+                    act(c2(tab, dst0 + a, dst0 + a + 512), ps, scale=0.0625)
+                else:
+                    ts(c2(tab, dst0 + a, dst0 + a + 512), ps, 0.0625, None, A.mult)
+    ends(0, 0)
+    shift("LO0", 0, 1024)
+    shift("HI0", 0, 1024)
+    ends(2048, 1024)
+    ends(4096, 2048)
+    act(ap("FM"), ap("FS"), scale=0.0625, bias=-1.0 / 128)
+    act(ap("FS"), ap("FS"), scale=0.0625)
+
+    def tables(par):
+        sp = ap("SP%d" % par)
+        ts(ap("DH"), sp, RND64, -RND64, A.add, A.add)
+        tt(ap("DL"), sp, ap("DH"), A.subtract)
+        for half in range(2):
+            for r in range(8 * half, 8 * half + 8):
+                o = c2("PI", r % 8, 512, 8)
+                mm([(o, c2("ZM", 144 * r + 16 - q, 144 * r + 144 - q),
+                     c2("DL" if q % 2 else "DH", 64 * (q // 2), 64 * (q // 2) + 64), q == 0, q == 9) for q in range(10)])
+            act(ap("SG", slice(None), slice(None), slice(8 * half, 8 * half + 8)), ap("PI"))
+        for kk in range(2):
+            a = 512 * (par + 2 * kk)
+            for x in ("ST", "RT"):
+                dma(c2(x, a, a + 512), ap("SG", slice(None), slice(32 * kk, 32 * kk + 32)))
+
+    def pick(out, j, w, extra=()):
+        it = [(out, c2("YM", 144 * j + 16 - r, 144 * j + 144 - r), c2("GB", r, 16 * w, 16), r == 0, r == 15 and not extra)
+              for r in range(16)]
+        mm(it + list(extra))
+
+    def chunk(t, k):
+        par = t % 2
+        kk, h = k // 2, k % 2
+        c = 4 * t + k
+        lo, hi, nlo, nhi = "LO%d" % par, "HI%d" % par, "LO%d" % (1 - par), "HI%d" % (1 - par)
+        gl, gh, ind, ks = "GL%d" % (c % 4), "GH%d" % (c % 4), "IN%d" % (c % 2), "KA" if c % 2 == 0 else "KB"
+        kc, rb, zb, na = "KC%d" % (c % 2), "RB%d" % (c % 2), "ZB%d" % (c % 2), "NA%d" % (c % 2)
+        le, lt = "LE%d" % (c % 2), "LT%d" % (c % 2)
+        v0 = 512 * (par + 2 * kk) + 256 * h
+
+        def blk(name, i, w=1, base=0):
+            return c2(name, base + 256 * i, base + 256 * (i + w))
+        dma(blk(gl, 4), c2(lo, v0, v0 + 256))
+        dma(blk(gh, 4), c2(hi, v0, v0 + 256))
+        for tab, dst in ((lo, gl), (hi, gh)):
+            for j in range(4):
+                o = 32 * j + 128 * kk + 16 * h
+                mine = k == 0 and j >= OPT["g0"] and (tab == hi or t == 0)
+                gather("dve" if mine else "act", blk(dst, j), ap(tab), c2("SU%d" % par, o, o + 16))
+        kq = ks
+        if OPT["sep"]:
+            kq, ks = "KA", "KB"
+        mn = blk(kq, 5)
+        for i, w in ((0, 2), (2, 2), (4, 1)):
+            if k == 0 and OPT["pe0"]:
+                mm([(blk(kq, i, w), idf, blk(gl, i, w), True, True)])
+            else:
+                act(blk(kq, i, w), blk(gl, i, w))
+        cuts = (0, 2, 4, 5) if k in OPT["split"] else OPT["cuts"]
+        for a, b in zip(cuts[:-1], cuts[1:]):
+            for s, (rot, src) in enumerate(((1, gl), (2, gl), (1, gh), (2, gh), (3, gh), (4, gh))):
+                for x, y, wrap in ((a, min(b, 5 - rot), False), (max(a, 5 - rot), b, True)):
+                    if y > x:
+                        op = A.is_ge if (wrap and src == gl) else A.is_gt
+                        tt(blk(ind, x, y - x, 1280 * s), blk(kq, x, y - x), blk(src, (x + rot) % 5, y - x), op)
+        back = {0: [(0, 1, 4, 0), (1, 1, 0, 0), (0, 2, 3, 1)], 2: [(2, 2, 1, 0), (2, 2, 0, 1)], 4: [(4, 1, 3, 0), (4, 1, 2, 1)]}
+        pre = OPT["presum"] and k not in OPT["short"]
+        if pre:
+            dma(c2(ind, 2560, 3840), c2(ind, 3840, 5120), accum=True)
+            dma(c2(ind, 5120, 6400), c2(ind, 6400, 7680), accum=True)
+        for i, w in ((0, 2), (2, 2), (4, 1)):
+            fw = ([(blk(ks, i, w), idf, blk(gl, i, w), True, False)]
+                  + [(blk(ks, i, w), idb if s < 2 else idn, blk(ind, i, w, 1280 * s), False, False)
+                     for s in ((0, 1, 2, 4) if pre else range(6))])
+            bw = [(blk(ks, x, ww), idn, blk(ind, y, ww, 1280 * s), False, (x, ww, y, s) == back[i][-1])
+                  for x, ww, y, s in back[i]]
+            if i == 4:
+                mm(fw + bw)
+            elif OPT["sep"]:
+                mm(fw[:1])
+                mm(fw[1:4])
+                mm(fw[4:])
+                mm(bw)
+            else:
+                mm(fw)
+                mm(bw)
+        boost[0] = OPT["tail"][k]
+        act(ap(kc), blk(ks, 0, 2))
+        tt(ap(kc), blk(ks, 2, 2), ap(kc), A.max)
+        sp_ = blk(ks, 5)
+        tt(sp_, blk(ks, 4), blk(kc, 0), A.max)
+        tt(sp_, sp_, blk(kc, 1), A.max)
+        short = k in OPT["short"]
+        if short or not OPT["ract"]:
+            ts(ap(rb), sp_, RND1, -RND1, A.add, A.add)
+        else:
+            act(ap(rb), sp_, bias=RND1)
+            act(ap(rb), ap(rb), bias=-RND1)
+        newlo, newhi = c2(nlo, v0, v0 + 256), c2(nhi, v0, v0 + 256)
+        if short:
+            tt(sp_, sp_, ap(rb), A.subtract)
+            if t < 3:
+                act(newlo, sp_, bias=-1.0 / 128)
+            else:
+                act(ap("AS"), sp_)
+            for j in range(5):
+                tt(blk(lt, j), sp_, blk(gh, j), A.is_gt)
+            dma(ap(gh), ap(lt), accum=True)
+            for j in range(4):
+                tt(blk(le, j), sp_, blk(gl, j), A.is_ge)
+            if OPT["sep"]:
+                act(mn, blk(gh, 0))
+                for j in range(1, 4):
+                    tt(mn, mn, blk(gh, j), A.min)
+                last = blk(gh, 4)
+            else:
+                act(blk(ks, 4, 2), blk(gh, 0, 2))
+                tt(blk(ks, 4, 2), blk(ks, 4, 2), blk(gh, 2, 2), A.min)
+                tt(ap(zb), blk(ks, 4), blk(gh, 4), A.min)
+                last = ap(zb)
+            if t < 3:
+                tt(newhi, mn, last, A.min)
+            else:
+                tt(mn, mn, last, A.min)
+                tt(ap(zb), mn, ap("AS"), A.add)
+                tt(ap(rb), mn, ap("AS"), A.subtract)
+                act(newlo, ap(zb), scale=8.0, bias=0.1875)
+                act(newhi, ap(rb), scale=8.0, bias=0.0625)
+        else:
+            tt(blk(na, 0), ap(rb), sp_, A.subtract)
+            if OPT["nadma"]:
+                for j in range(1, 5):
+                    dma(blk(na, j), blk(na, 0))
+            else:
+                acts([(blk(na, j), blk(na, 0)) for j in range(1, 5)])
+            dma(ap(gh), ap(na), accum=True)
+            dma(blk(gl, 0, 4), blk(na, 0, 4), accum=True)
+            if t < 3:
+                act(newlo, blk(na, 0), scale=-1.0, bias=-1.0 / 128)
+                act(newhi, blk(na, 0), scale=-1.0, bias=1.0)
+            else:
+                act(newlo, blk(na, 0), scale=-16.0, bias=0.125)
+            act(ap(lt), ap(gh), scale=-1.0, bias=-2.0 ** -21, func=AF.Sign)
+            dma(ap(gh), ap(lt), accum=True)
+            act(ap(le), blk(gl, 0, 4), scale=-1.0, bias=2.0 ** -21, func=AF.Sign)
+            act(mn, blk(gh, 0))
+            for j in range(1, 4):
+                tt(mn, mn, blk(gh, j), A.min)
+            tt(ap(zb), mn, blk(gh, 4), A.min)
+            if t < 3:
+                dma(newhi, ap(zb), accum=True)
+            else:
+                act(newhi, ap(zb), scale=8.0, bias=8.0625)
+                dma(newlo, newhi, accum=True)
+        boost[0] = 0.0
+        o = c2("PL", 64 * k, 64 * k + 64)
+        u0 = 144 if short else 0
+        it = []
+        for r in range(16):
+            it.append((o, c2("UP", u0 + 16 - r, u0 + 144 - r), c2(le, r, 1024, 16), r == 0, False))
+            it.append((o, c2("UN", u0 + 16 - r, u0 + 144 - r), c2(lt, r, 1024, 16), False, False))
+        it.append((o, idb, ap("CJ"), False, False))
+        it.append((o, idf, ap("SP%d" % par, slice(None), slice(0, 4), kk, slice(16 * h, 16 * h + 16)), False, True))
+        mm(it)
+        act(ap("KS%d" % par, slice(None), slice(None), kk, slice(16 * h, 16 * h + 16)), o)
+
+    def drift(t):
+        par = t % 2
+        lo, hi, nlo, nhi = "LO%d" % par, "HI%d" % par, "LO%d" % (1 - par), "HI%d" % (1 - par)
+        for kk in range(2):
+            a = 512 * (1 - par + 2 * kk)
+            if t < 3:
+                dma(c2(nlo, a, a + 512), c2(lo, a, a + 512))
+                dma(c2(nhi, a, a + 512), c2(hi, a, a + 512))
+                dma(c2(nlo, a, a + 512), c2("FM", a, a + 512), accum=True)
+                dma(c2(nhi, a, a + 512), c2("FS", a, a + 512), accum=True)
+            else:
+                tmp = c2("TMP", 512 * kk, 512 * kk + 512)
+                act(c2(nlo, a, a + 512), c2(lo, a, a + 512), scale=8.0, bias=0.1875)
+                act(c2(nhi, a, a + 512), c2(lo, a, a + 512), scale=-8.0, bias=0.0625)
+                act(tmp, c2(hi, a, a + 512), scale=8.0)
+                dma(c2(nlo, a, a + 512), tmp, accum=True)
+                dma(c2(nhi, a, a + 512), tmp, accum=True)
+                dma(c2(nlo, a, a + 512), c2("dr", a, a + 512), accum=True)
+            if kk == 0:
+                publish([nlo, nhi], a, 512)
+
+    def elect(t, k0, nk):
+        par = t % 2
+        spn, vc, ksn = "SP%d" % par, "VC%d" % par, "KS%d" % par
+        w, al, q = 32 * nk, slice(None), slice(k0, k0 + nk)
+        boost[0] = OPT["boost"]
+
+        def sm(i):
+            return c2("SM", 64 * i, 64 * i + w)
+
+        def ix(i):
+            return c2("IX", 64 * i, 64 * i + w)
+        some, meet, take, d, kv, o1, o2, off, lim, nm = [sm(i) for i in range(10)]
+        rr, rows = ap(spn, al, 4, q), ap(spn, al, slice(0, 4), q)
+        kt, ca, gb = c2("KT", 0, w), c2("CA", 0, w), c2("GB", 0, 16 * w)
+        keep, new, ok, stay = c2("PI", 0, 4 * w), c2("PI", 256, 256 + 4 * w), c2("OK", 0, 4 * w), c2("STAY", 0, 4 * w)
+        tt(c2("M2", 0, 2 * w), ap(ksn, al, slice(0, 2), q), ap(ksn, al, slice(2, 4), q), A.max)
+        tt(kt, c2("M2", 0, w), c2("M2", w, 2 * w), A.max)
+        ts(ca, kt, 4095, None, A.bitwise_and)
+        ts(ix(0), ca, 2048.0, None, A.min)
+        ts(some, kt, float(THR), None, A.is_ge)
+        tt(c2("EQ", 0, w), ca, ap(vc, al, 0, q), A.is_equal)
+        ts(stay, ap(ksn, al, al, q), float(THR), None, A.is_ge)
+        tt(d, ca, rr, A.subtract)
+        for m in range(3):
+            gather("act", gb, ap("RT"), ix(m))
+            hm = c2("PL", 256 + w * m, 256 + w * (m + 1))
+            pick(hm, 4, w)
+            if m < 2:
+                ts(ix(m + 1), hm, 2048.0, None, A.min)
+        tt(c2("EQ", w, 4 * w), c2("PL", 256, 256 + 3 * w), ap(vc, al, slice(1, 4), q), A.is_equal)
+        tt(c2("M2", 0, 2 * w), c2("EQ", 0, 2 * w), c2("EQ", 2 * w, 4 * w), A.max)
+        tt(meet, c2("M2", 0, w), c2("M2", w, 2 * w), A.max)
+        tt(take, some, meet, A.is_gt)
+        tt(d, d, take, A.mult)
+        tt(rr, rr, d, A.add)
+        cp(ix(3), rr)
+        gather("act", gb, ap("ST"), ix(3))
+        if t < 3:
+            credit([c2("ST", 2048 + 512 * par, 2560 + 512 * par)])
+        ts(o1, rr, 2048.0, 2048.0, A.is_ge, A.mult)
+        ts(o2, rr, 3072.0, 1024.0, A.is_ge, A.mult)
+        tt(off, o1, o2, A.add)
+        act(nm, meet, scale=-1048576.0, bias=1048576.0)
+        tt(kv, kt, nm, A.add)
+        act(lim, o1, scale=-0.5, bias=4096.0)
+        tt(lim, lim, o2, A.add)
+        for j in range(4):
+            tt(c2("PI", w * j, w * j + w), ap(ksn, al, j, q), kv, A.is_lt)
+        tt(keep, keep, stay, A.mult)
+        for j in range(4):
+            o = c2("PI", 256 + w * j, 256 + w * j + w)
+            pick(o, j, w, [(o, idf, off, False, True)])
+        for j in range(4):
+            tt(c2("OK", w * j, w * j + w), c2("PI", 256 + w * j, 256 + w * j + w), lim, A.is_lt)
+        tt(new, new, rows, A.subtract)
+        tt(ok, keep, ok, A.is_lt)
+        tt(new, new, ok, A.mult)
+        tt(rows, new, rows, A.add)
+        for kk in range(k0, k0 + nk):
+            cp(c2("SU%d" % par, 128 * kk, 128 * kk + 128), ap(spn, al, slice(0, 4), kk))
+        if t >= 2:
+            cp(ap("RF", al, q, par), rr)
+        if t < 3:
+            tables(par)
+            publish(["ST"], 512 * par, 512)
+        boost[0] = 0.0
+
+    tables(0)
+    tables(1)
+    publish(["ST"], 0, 1024)
+    for t in range(4):
+        par = t % 2
+        drift(t)
+        for k in range(4):
+            chunk(t, k)
+            if k == 1:
+                publish(["LO%d" % (1 - par)], 512 * par, 512)
+                publish(["HI%d" % (1 - par)], 512 * par, 512)
+                if t == 3:
+                    elect(3, 0, 1)
+        if t < 3:
+            credit([c2("LO%d" % par, 2048, 3072), c2("HI%d" % par, 2048, 3072)])
+            elect(t, 0, 2)
+        else:
+            elect(3, 1, 1)
+
+    dma(ap("yt"), c2("LO0", 0, 2048))
+    add("pe", "c", lambda e: [e.transpose(T["PI"][:, 0:128], T["RF"][:], T["IDF"][:])], [ap("RF"), idf],
+        [c2("PI", 0, 128)], 300.0, 60)
+    act(ap("RFT"), c2("PI", 0, 128))
+    for gi in range(8):
+        dma(ap("yr", gi), c2("RFT", 16 * gi, 16 * gi + 16))
+    for s, a in enumerate((0, 2, 1, 3)):
+        par, kk, zo = a % 2, a // 2, 2048 * (s % 2)
+        own = c2("FM", 512 * a, 512 * a + 512)
+        dma(own, c2("LO0", 512 * a, 512 * a + 512))
+        ps = c2("KA" if s % 2 == 0 else "KB", 0, 512)
+        mm([(ps, idh, c2("HI0", 512 * a, 512 * a + 512), True, False)])
+        for j in range(4):
+            off = c2("SU%d" % par, 32 * j + 128 * kk, 32 * j + 128 * kk + 32)
+            z = c2("LO1", zo + 512 * j, zo + 512 * j + 512)
+            p = c2("HI1", zo + 512 * j, zo + 512 * j + 512)
+            if j >= OPT["fin"][s]:
+                gather("act", z, ap("LO0"), off, scale=-1.0)
+                dma(z, own, accum=True)
+                act(z, z, scale=-1.0, func=AF.Sigmoid)
+            else:
+                gather("dve", z, ap("LO0"), off, other=own, op=A.subtract)
+                act(z, z, func=AF.Sigmoid)
+            gather("dve", p, ap("HI0"), off, other=z, op=A.mult)
+            mm([(ps, idf, p, False, j == 3)])
+        act(ap("YB%d" % (s % 2)), ps)
+        dma(c2("yq", 512 * a, 512 * a + 512), ap("YB%d" % (s % 2)))
+    return ops
+
+
+def schedule(ops):
+    n = len(ops)
+    real = ops
+    ops = [dict(o) for o in real]
+    for o in ops:
+        if o["kind"] == "d":
+            o["lat"] = 1800 + (o["lat"] - 1800) * OPT["ds"]
+            o["dur"] *= OPT["ds"]
+        elif o["kind"] == "r":
+            o["lat"] *= OPT["rs"]
+        elif o["eng"] == "pe":
+            o["dur"] *= OPT["ps"]
+        elif o.get("gat"):
+            o["dur"] *= OPT["gs"]
+    succ = [[] for _ in range(n)]
+    pred = [sorted(set(d for d, w in o["deps"])) for o in ops]
+    for i in range(n):
+        for d in pred[i]:
+            succ[d].append(i)
+
+    def sweep(before, after, prio, back):
+        left = [len(p) for p in before]
+        free, bfree, blast, dfree = {}, {}, {}, 0.0
+        start, done = [0.0] * n, [0.0] * n
+        rdy = [o["lat"] if back else 0.0 for o in ops]
+        ready = set(i for i in range(n) if left[i] == 0)
+        order, extra = [], []
+        while ready:
+            est = {}
+            for i in ready:
+                o = ops[i]
+                s = max(rdy[i], free.get(o["eng"], 0.0))
+                for b in o["banks"]:
+                    if b in blast and ops[blast[b]]["eng"] != o["eng"]:
+                        s = max(s, bfree[b] + HOP)
+                est[i] = s
+            first = min(ready, key=lambda i: (est[i], -prio[i], i))
+            e = ops[first]["eng"]
+            i = max((x for x in ready if ops[x]["eng"] == e and est[x] <= est[first] + OPT["look"]),
+                    key=lambda x: (prio[x], -x))
+            o = ops[i]
+            start[i] = est[i]
+            free[e] = est[i] + o["dur"]
+            done[i] = free[e] + (0.0 if back else o["lat"])
+            if o["kind"] == "d" and not back:
+                done[i] = max(done[i], dfree + o["lat"] - 1800)
+                dfree = done[i]
+            for b in o["banks"]:
+                if b in blast and ops[blast[b]]["eng"] != e:
+                    extra.append((i, blast[b]))
+                blast[b] = i
+                bfree[b] = done[i]
+            ready.discard(i)
+            order.append(i)
+            for s in after[i]:
+                rdy[s] = max(rdy[s], done[i] + HOP + (ops[s]["lat"] if back else 0.0))
+                left[s] -= 1
+                if left[s] == 0:
+                    ready.add(s)
+        return order, start, done, extra
+
+    prio = [0.0] * n
+    for i in range(n - 1, -1, -1):
+        prio[i] = ops[i]["dur"] + ops[i]["lat"] + max([prio[s] + HOP for s in succ[i]] + [0.0])
+    base = list(prio)
+    prio = [p + o["boost"] for p, o in zip(prio, ops)]
+    best = None
+    for turn in range(OPT["turns"]):
+        fw = sweep(pred, succ, prio, False)
+        if best is None or max(fw[2]) < max(best[2]):
+            best = fw
+        late = sweep(succ, pred, fw[2], True)[2]
+        prio = [OPT["mix"] * a + (1 - OPT["mix"]) * b for a, b in zip(late, prio if turn else base)]
+    return best
+
+
+def rank_program(g, core, T, topo):
+    if T.rank_of(core) is None:
+        return
+    ops = build(g, core, T, topo)
+    key = repr(sorted(OPT.items()))
+    if key not in LAST:
+        LAST[key] = schedule(ops)
+    order, start, done, extra = LAST[key]
+    for i, d in extra:
+        ops[i]["deps"].add((d, "W"))
+    LAST["plan"] = (ops, order, start, done)
+    queue = {"pe": g.tensor, "dve": g.vector, "act": g.scalar, "pool": g, "sync": g.sync}
+    known = {q: {} for q in queue}
+    total, waited, when = {}, {}, {}
+    pools = {"pool": [["dg%d" % k, None] for k in range(NG)], "sync": [["ds%d" % k, None] for k in range(NS)]}
+
+    def wait(q, tok):
+        sem, cnt, snap = tok
+        if known[q].get(sem, 0) >= cnt:
+            return False
+        queue[q].wait_ge(T.sem[sem], cnt)
+        waited[sem] = max(waited.get(sem, 0), cnt)
+        known[q][sem] = cnt
+        for s, v in snap.items():
+            if known[q].get(s, 0) < v:
+                known[q][s] = v
+        return True
+
+    def need(q, d, w, i):
+        tok = ops[d]["tok" + w]
+        if known[q].get(tok[0], 0) >= tok[1]:
+            return
+        if ops[d].get("reused"):
+            need(q, ops[d]["waiters"][0], "R", i)
+        elif wait(q, tok) and ops[d]["kind"] == "d":
+            ops[d]["waiters"].append(i)
+
+    for i in order:
+        o = ops[i]
+        q = o["eng"]
+        for d, w in sorted(o["deps"], key=lambda x: (-done[x[0]], x)):
+            need(q, d, w, i)
+        if o["kind"] == "c":
+            sem = "e_" + q
+            for ins in o["emit"](queue[q]):
+                ins.then_inc(T.sem[sem], 1)
+                total[sem] = total.get(sem, 0) + 1
+            o["tokR"] = o["tokW"] = (sem, total[sem], dict(known[q]))
+        elif o["kind"] == "d":
+            slot = [s for s in pools[q] if s[1] is None or [w for w in ops[s[1]]["waiters"] if w != i]][0]
+            if slot[1] is not None:
+                for w in list(ops[slot[1]]["waiters"]):
+                    if ops[w]["eng"] != q:
+                        need(q, w, "R", i)
+                ops[slot[1]]["reused"] = True
+            pools[q].remove(slot)
+            pools[q].append(slot)
+            slot[1] = i
+            sem = slot[0]
+            o["waiters"] = []
+            o["emit"](queue[q])[0].then_inc(T.sem[sem], 16)
+            total[sem] = total.get(sem, 0) + 16
+            o["tokR"] = o["tokW"] = (sem, total[sem], dict(known[q]))
+        else:
+            k, cnt = o["rem"]
+            o["emit"](queue[q])
+            total["rl%d" % k] = total["rr%d" % k] = cnt
+            when["rr%d" % k] = done[i]
+            sem = "rl%d" % k
+            o["tokR"] = (sem, cnt, dict(known[q]))
+            o["tokW"] = ("rr%d" % k, cnt, {})
+        when[sem] = done[i]
+    for sem in sorted(total, key=lambda s: when[s]):
+        if waited.get(sem, 0) < total[sem]:
+            g.wait_ge(T.sem[sem], total[sem])

@@ -2,121 +2,150 @@ from concourse.bass import DstId, RemoteDMATransfer
 from concourse.mybir import AluOpType, ActivationFunctionType
 
 F, B, I, U = "float32", "bfloat16", "int32", "uint16"
-NG, NS, NR = 30, 68, 24
+NG, NS, NL, NR = 24, 47, 22, 52
 SCRATCH = {
     "LO0": ("sbuf", [128, 4096], F), "LO1": ("sbuf", [128, 4096], F),
     "HI0": ("sbuf", [128, 4096], F), "HI1": ("sbuf", [128, 4096], F),
-    "ST": ("sbuf", [128, 4096], B), "RT": ("sbuf", [128, 2064], B),
-    "FM": ("sbuf", [128, 2048], F), "FS": ("sbuf", [128, 2048], B), "AS": ("sbuf", [128, 256], F),
-    "TMP": ("sbuf", [128, 1024], F), "ZM": ("sbuf", [128, 2304], B),
-    "SLI": ("sbuf", [128, 4, 4, 32], I), "RFI": ("sbuf", [128, 2, 2, 32], I), "RF": ("sbuf", [128, 2, 2, 32], F),
-    "RFT": ("sbuf", [128, 128], F), "SG": ("sbuf", [128, 64, 16], B),
-    "XI": ("sbuf", [128, 144], F), "XD": ("sbuf", [128, 128], F),
-    "IDB": ("sbuf", [128, 128], B), "IDN": ("sbuf", [128, 128], B), "IDF": ("sbuf", [128, 128], F),
-    "IDH": ("sbuf", [128, 128], F),
-    "UP": ("sbuf", [128, 288], B), "UN": ("sbuf", [128, 288], B), "YM": ("sbuf", [128, 720], B),
-    "PC": ("sbuf", [128, 8], I), "PF": ("sbuf", [128, 32], F),
-    "VC0": ("sbuf", [128, 4, 2, 32], F), "VC1": ("sbuf", [128, 4, 2, 32], F), "CJ": ("sbuf", [128, 64], B),
-    "KS0": ("sbuf", [128, 4, 2, 32], F), "KS1": ("sbuf", [128, 4, 2, 32], F), "M2": ("sbuf", [128, 128], F), "KT": ("sbuf", [128, 64], I),
-    "CA": ("sbuf", [128, 64], I), "IX": ("sbuf", [128, 256], U), "SM": ("sbuf", [128, 640], F),
-    "EQ": ("sbuf", [128, 256], F), "STAY": ("sbuf", [128, 256], F), "OK": ("sbuf", [128, 256], F),
-    "DH": ("sbuf", [128, 320], B), "DL": ("sbuf", [128, 320], B), "GB": ("sbuf", [128, 1024], B),
+    "ST": ("sbuf", [128, 4096], B),
+    "FM": ("sbuf", [128, 3072], F), "FS": ("sbuf", [128, 3072], F), "IN1": ("sbuf", [128, 10240], B), "AS": ("sbuf", [128, 512], F),
+    "YM": ("sbuf", [128, 720], B), "UP": ("sbuf", [128, 288], B), "UN": ("sbuf", [128, 288], B),
+    "SLI": ("sbuf", [128, 4, 4, 32], I), "RFI": ("sbuf", [128, 2, 2, 32], I), "RR": ("sbuf", [128, 2, 2, 32], F),
+    "RFT": ("sbuf", [128, 128], F), "XI": ("sbuf", [128, 144], F), "XD": ("sbuf", [128, 128], F),
+    "N1": ("sbuf", [128, 128], B), "NH": ("sbuf", [128, 128], B),
+    "P1": ("sbuf", [128, 128], B), "W12": ("sbuf", [128, 128], B), "W20": ("sbuf", [128, 128], B),
+    "IDF": ("sbuf", [128, 128], F), "IDN": ("sbuf", [128, 128], F), "ID4": ("sbuf", [128, 128], F), "ID8": ("sbuf", [128, 128], F),
+    "PC": ("sbuf", [128, 8], I), "PF": ("sbuf", [128, 32], F), "VI": ("sbuf", [128, 256], F),
+    "CJ": ("sbuf", [128, 128], B), "TJ": ("sbuf", [128, 256], B), "WS": ("sbuf", [128, 512], B),
+    "XT": ("sbuf", [128, 32, 32], B), "XU0": ("sbuf", [128, 32, 32], B), "XU1": ("sbuf", [128, 32, 32], B), "M2": ("sbuf", [128, 128], F),
+    "IX": ("sbuf", [128, 256], U), "SM": ("sbuf", [128, 320], F), "SB": ("sbuf", [128, 320], B),
+    "CM": ("sbuf", [128, 256], B), "N4": ("sbuf", [128, 4, 512], F), "EQ": ("sbuf", [128, 256], B), "STAY": ("sbuf", [128, 256], B), "NV": ("sbuf", [128, 256], B),
+    "THR": ("sbuf", [128, 256], F), "CH": ("sbuf", [128, 256], F),
+    "GB": ("sbuf", [128, 1024], B),
     "KA": ("psum", [128, 1536], F), "KB": ("psum", [128, 1536], F),
-    "PL": ("psum", [128, 512], F), "PI": ("psum", [128, 512], F),
+    "PL": ("psum", [128, 512], F), "PI": ("psum", [128, 16, 32], F),
 }
-for _k in range(4):
-    SCRATCH["GL%d" % _k] = ("sbuf", [128, 1280], F)
-    SCRATCH["GH%d" % _k] = ("sbuf", [128, 1280], F)
 for _k in range(2):
-    SCRATCH["IN%d" % _k] = ("sbuf", [128, 7680], B)
-    SCRATCH["LE%d" % _k] = ("sbuf", [128, 1024], B)
-    SCRATCH["LT%d" % _k] = ("sbuf", [128, 1280], B)
+    SCRATCH["GL%d" % _k] = ("sbuf", [128, 4, 512], F)
+    SCRATCH["GH%d" % _k] = ("sbuf", [128, 2, 5, 256], F)
+    SCRATCH["LE%d" % _k] = ("sbuf", [128, 2, 4, 256], B)
+    SCRATCH["LT%d" % _k] = ("sbuf", [128, 2, 5, 256], B)
+    SCRATCH["NA%d" % _k] = ("sbuf", [128, 512], F)
     SCRATCH["KC%d" % _k] = ("sbuf", [128, 512], F)
+    SCRATCH["OL%d" % _k] = ("sbuf", [128, 256], F)
     SCRATCH["RB%d" % _k] = ("sbuf", [128, 256], F)
-    SCRATCH["ZB%d" % _k] = ("sbuf", [128, 256], F)
-    SCRATCH["NA%d" % _k] = ("sbuf", [128, 1280], F)
-    SCRATCH["SP%d" % _k] = ("sbuf", [128, 5, 2, 32], F)
+    SCRATCH["SP%d" % _k] = ("sbuf", [128, 4, 2, 32], F)
+    SCRATCH["KS%d" % _k] = ("sbuf", [128, 4, 2, 32], F)
+    SCRATCH["VC%d" % _k] = ("sbuf", [128, 4, 2, 32], F)
     SCRATCH["SU%d" % _k] = ("sbuf", [128, 256], U)
     SCRATCH["YB%d" % _k] = ("sbuf", [128, 512], F)
 SEMAPHORES = (["e_pe", "e_dve", "e_act", "e_pool"] + ["dg%d" % k for k in range(NG)] + ["ds%d" % k for k in range(NS)]
-              + ["rl%d" % k for k in range(NR)] + ["rr%d" % k for k in range(NR)])
+              + ["bl"] + ["rl%d" % k for k in range(NL)] + ["rr%d" % k for k in range(NR)])
 
-CY, PCY, GA, HOP = 1.0, 0.5, 1.56, 120.0
-THR = 9 * 16384
+CY, PCY, GA, HOP = 0.92, 0.46, 1.56, 120.0
 RND1 = 1.5 * 2.0 ** 23
-RND64 = 1.5 * 2.0 ** 29
+RND12 = 1.5 * 2.0 ** 35
+MID = 2047.5
 SIZE = {F: 4, I: 4, B: 2, U: 2}
 LAST = {}
-OPT = {"boost": 3000.0, "ract": True, "g0": 3, "fin": (2, 2, 2, 2), "look": 50.0, "tail": (0.0, 0.0, 0.0, 0.0),
-       "nadma": False, "cuts": (0, 2, 5), "short": (1, 3), "turns": 6, "mix": 0.5,
-       "ds": 1.2, "rs": 1.0, "ps": 1.0, "gs": 1.1,
-       "split": (0, 3), "sep": True, "pe0": True, "presum": False}
+SPEEDS = ((1, 1, 1, 0.87, 0.87, 0.87, 0.95, 60), (0.7, 1, 1, 1.25, 1.25, 1.25, 0.95, 60), (0.7, 1, 1, 1.05, 1.05, 1.05, 1.33, 60),
+          (0.7, 1, 1, 0.87, 0.87, 1.3, 1, 60), (0.7, 2.2, 1, 0.87, 0.87, 0.87, 1, 200), (1.6, 1.2, 1, 0.87, 0.87, 0.87, 1, 60),
+          (1, 1.3, 4, 0.87, 0.87, 0.87, 1, 100), (0.7, 1, 1, 0.87, 0.87, 0.87, 1, 400), (0.7, 1, 1, 0.87, 1.2, 0.87, 1, 60))
+WEIGHTS = (1, 2, 2, 1, 2, 0.5, 0.5, 1.5, 1)
+OPT = {"boost": 1500.0, "vg": 3, "vg0": 4, "fin": (2, 2, 2, 2, 4), "edge": 2000.0, "turns": 5, "mix": 0.6,
+       "cuts": (((0, 2), (2, 5)),) * 4, "vround": (3,), "pelo": (), "kinds": ("FEEP", "FEEP", "FEEP", "EEEP"),
+       "fsum": (), "pair": False, "end": 6000.0, "mend": 15, "step": 1000.0, "back": 10, "early": 20000.0, "last": 2.0,
+       "tries": (((1.0, 2.0, 1.5, 1, 1.1, 1.15, 1.15, 150), 30.0, 0.0, 0.5),),
+       "here": 6, "relay": "", "many": 2, "wide": False, "keep": 0.5, "vle": ((3, 2), (3, 3))}
 
 
-def build(g, core, T, topo):
+def neighbours(core, T, topo):
+    down = T.cores[(T.rank_of(core) - 1) % len(T.cores)]
+    free = [c for c in topo.cores_of(core) if T.rank_of(c) is None and topo.die(c) == topo.die(core)]
+    first = [c for c in free if topo.may_write(c, down)][0]
+    return [first, [c for c in free if c != first][0]]
+
+
+def build(core, T, topo, lite=False):
     A = AluOpType
     AF = ActivationFunctionType
     n = len(T.cores)
     rank = T.rank_of(core)
     down, up = T.cores[(rank - 1) % n], T.cores[(rank + 1) % n]
+    mates = neighbours(core, T, topo)
     ops = []
     hist = {}
-    boost = [0.0]
+    boost, gate = [0.0], [None]
+    al = slice(None)
 
     def ap(name, *idx):
         shape = list(T[name].shape)
-        idx = list(idx) + [slice(None)] * (len(shape) - len(idx))
-        lo, hi, cnt, stride, pr = 0, 0, 1, 1, None
+        idx = list(idx) + [al] * (len(shape) - len(idx))
+        runs, cnt, stride, pr, full = [(0, 1)], 1, 1, None, True
         for d in range(len(shape) - 1, -1, -1):
             x = idx[d]
             r = range(x, x + 1) if isinstance(x, int) else range(*x.indices(shape[d]))
             if d == 0:
                 pr = (r[0], r[-1] + 1)
+                break
+            cnt *= len(r)
+            if len(runs) == 1 and runs[0] == (0, stride) and r.step == 1:
+                runs = [(r[0] * stride, (r[-1] + 1) * stride)]
+            elif len(runs) * len(r) <= 8:
+                runs = [(a + i * stride, b + i * stride) for i in r for a, b in runs]
             else:
-                lo += r[0] * stride
-                hi += r[-1] * stride
-                cnt *= len(r)
-                stride *= shape[d]
+                runs, full = [(runs[0][0] + r[0] * stride, runs[-1][1] + r[-1] * stride)], False
+            stride *= shape[d]
         where, dtype = (SCRATCH[name][0], SCRATCH[name][2]) if name in SCRATCH else ("dram", F)
-        return {"a": T[name][tuple(idx)], "n": name, "p": pr, "lo": lo, "hi": hi + 1, "cnt": cnt,
+        return {"a": T[name][tuple(idx)], "n": name, "p": pr, "runs": runs, "full": full, "cnt": cnt,
                 "ps": where == "psum", "sz": SIZE[dtype]}
 
-    def c2(name, a, b, step=1):
-        return ap(name, slice(None), slice(a, b, step))
+    def c2(name, a, b, step=1, part=al):
+        shape, idx = list(T[name].shape)[1:], [part]
+        for d in range(len(shape)):
+            inner = 1
+            for x in shape[d + 1:]:
+                inner *= x
+            if d == len(shape) - 1:
+                idx.append(slice(a, b, step))
+            elif a // inner == (b - 1) // inner:
+                idx.append(a // inner)
+                a, b = a % inner, (b - 1) % inner + 1
+            else:
+                idx.append(slice(a // inner, b // inner))
+                break
+        return ap(name, *idx)
 
-    def add(eng, kind, emit, R, W, dur, lat=0.0):
+    def add(eng, kind, emit, R, W, dur, lat=0.0, X=()):
         me = len(ops)
         deps = set()
-        for acc, wr in [(x, False) for x in R] + [(x, True) for x in W]:
-            for e in hist.get(acc["n"], []):
-                if e[0] < acc["hi"] and acc["lo"] < e[1] and e[2] < acc["p"][1] and acc["p"][0] < e[3] and e[4] != me:
-                    if e[5]:
-                        deps.add((e[4], "W"))
-                    elif wr:
-                        deps.add((e[4], "R"))
+        if lite:
+            ops.append({})
+            return me
+        if gate[0] is not None:
+            deps.add((gate[0], "W"))
+        for acc, wr in [(x, "") for x in R] + [(x, "W") for x in W] + [(x, "X") for x in X]:
             h = hist.setdefault(acc["n"], [])
-            if wr:
-                h[:] = [e for e in h if not (acc["lo"] <= e[0] and e[1] <= acc["hi"] and acc["p"][0] <= e[2]
-                                             and e[3] <= acc["p"][1] and acc.get("full", True))]
-            h.append((acc["lo"], acc["hi"], acc["p"][0], acc["p"][1], me, wr))
+            for e in h:
+                if e[4] != me and e[0] < acc["p"][1] and acc["p"][0] < e[1] and (e[5] or wr):
+                    if [1 for a, b in acc["runs"] if e[2] < b and a < e[3]]:
+                        deps.add((e[4], e[5] or "R"))
+            if wr and acc["full"]:
+                h[:] = [e for e in h if not (acc["p"][0] <= e[0] and e[1] <= acc["p"][1]
+                                             and [1 for a, b in acc["runs"] if a <= e[2] and e[3] <= b])]
+            h.extend((acc["p"][0], acc["p"][1], a, b, me, wr) for a, b in acc["runs"])
         banks = set()
         for acc in R + W:
             if acc["ps"]:
-                for b in range(acc["lo"] // 512, (acc["hi"] - 1) // 512 + 1):
-                    banks.add((acc["n"], b))
+                for a, b in acc["runs"]:
+                    for x in range(a // 512, (b - 1) // 512 + 1):
+                        banks.add((acc["n"], x))
         ops.append({"eng": eng, "kind": kind, "emit": emit, "deps": deps, "dur": dur, "lat": lat, "banks": banks,
-                    "tag": "%s:%d" % (W[0]["n"], W[0]["lo"]), "boost": boost[0]})
+                    "boost": boost[0]})
         return me
 
-    def part(x):
-        if x["cnt"] != x["hi"] - x["lo"]:
-            x = dict(x)
-            x["full"] = False
-        return x
-
-    def tt(out, a, b, op, win=None):
+    def tt(out, a, b, op):
         cyc = 1 if (a["ps"] or b["ps"]) else 2
-        add("dve", "c", lambda e: [e.tensor_tensor(out["a"], a["a"], b["a"], op)], [a, b], [part(out)],
+        add("dve", "c", lambda e: [e.tensor_tensor(out["a"], a["a"], b["a"], op)], [a, b], [out],
             50 + max(64, out["cnt"] * cyc) * CY)
 
     def ts(out, a, s1, s2, op0, op1=None):
@@ -129,27 +158,25 @@ def build(g, core, T, topo):
             if op1 is None:
                 return [e.tensor_scalar(out["a"], a["a"], v1, None, op0)]
             return [e.tensor_scalar(out["a"], a["a"], v1, v2, op0, op1)]
-        add("dve", "c", emit, R, [part(out)], 50 + max(64, out["cnt"] * half) * CY)
+        add("dve", "c", emit, R, [out], 50 + max(64, out["cnt"] * half) * CY)
 
     def cp(out, a):
-        add("dve", "c", lambda e: [e.tensor_copy(out["a"], a["a"])], [a], [part(out)], 50 + max(64, out["cnt"]) * CY)
+        add("dve", "c", lambda e: [e.tensor_copy(out["a"], a["a"])], [a], [out], 50 + max(64, out["cnt"]) * CY)
 
     def act(out, a, scale=1.0, bias=0.0, func=None):
         f = func if func is not None else (AF.Copy if bias == 0.0 else AF.Identity)
-        add("act", "c", lambda e: [e.activation(out["a"], a["a"], f, bias=bias, scale=scale)], [a], [part(out)],
+        add("act", "c", lambda e: [e.activation(out["a"], a["a"], f, bias=bias, scale=scale)], [a], [out],
             65 + max(64, out["cnt"]) * CY)
 
-    def acts(pairs):
-        add("act", "c", lambda e: [e.activation(o["a"], a["a"], AF.Copy) for o, a in pairs],
-            [a for o, a in pairs], [part(o) for o, a in pairs], sum(65 + max(64, o["cnt"]) * CY for o, a in pairs))
-
-    def gather(eng, out, win, off, scale=1.0, other=None, op=None):
+    def gather(eng, out, win, off, scale=1.0, bias=0.0, other=None, op=None):
         dur = 60 + out["cnt"] * GA * CY
         if eng == "act":
-            add("act", "c", lambda e: [e.activation(out["a"], win["a"].indirect(off["a"]), AF.Copy, scale=scale)],
+            f = AF.Copy if bias == 0.0 else AF.Identity
+            add("act", "c", lambda e: [e.activation(out["a"], win["a"].indirect(off["a"]), f, bias=bias, scale=scale)],
                 [win, off], [out], dur)
         elif other is None:
-            add("dve", "c", lambda e: [e.tensor_copy(out["a"], win["a"].indirect(off["a"]))], [win, off], [out], dur)
+            add("dve", "c", lambda e: [e.tensor_scalar(out["a"], win["a"].indirect(off["a"]), scale, bias, A.mult, A.add)],
+                [win, off], [out], dur)
         else:
             add("dve", "c", lambda e: [e.tensor_tensor(out["a"], win["a"].indirect(off["a"]), other["a"], op)],
                 [win, off, other], [out], dur)
@@ -159,9 +186,12 @@ def build(g, core, T, topo):
         R, W, dur = [], [], 0.0
         for o, l, r, st, sp in items:
             R += [l, r] + ([] if st else [o])
-            W.append(part(o))
+            W.append(o)
             dur += (max(64, r["cnt"]) * (4 if r["sz"] == 4 else 1) + 16) * PCY
         add("pe", "c", lambda e: [e.matmul(o["a"], l["a"], r["a"], st, sp) for o, l, r, st, sp in items], R, W, dur, 60)
+
+    def group(items, start=True):
+        mm([(o, l, r, start and k == 0, k == len(items) - 1) for k, (o, l, r) in enumerate(items)])
 
     def iota(out, pattern, base, mult):
         kw = {} if SCRATCH[out["n"]][2] == I else {"allow_small_or_imprecise_dtypes": True}
@@ -171,12 +201,12 @@ def build(g, core, T, topo):
         side = out if out["n"] in SCRATCH else a
         by = side["cnt"] * side["sz"] * (side["p"][1] - side["p"][0])
         if accum:
-            add("pool", "d", lambda e: [e.dma_start(out["a"], a["a"], accum_op=A.add)], [a, out], [part(out)],
+            add("pool", "d", lambda e: [e.dma_start(out["a"], a["a"], accum_op=A.add)], [a, out], [out],
                 900.0, 1800 + by / 300.0)
         else:
-            add("sync", "d", lambda e: [e.dma_start(out["a"], a["a"])], [a], [part(out)], 100.0, 1800 + by / 500.0)
+            add("sync", "d", lambda e: [e.dma_start(out["a"], a["a"])], [a], [out], 100.0, 1800 + by / 500.0)
 
-    nrem = [0]
+    nrem = [0, 0]
 
     def send(pairs):
         k = nrem[0]
@@ -190,30 +220,86 @@ def build(g, core, T, topo):
                                     dma_engine_mask=sum(1 << x for x in eng[j * per:(j + 1) * per]),
                                     remote_sem=T.sem["rr%d" % k], src=s["a"], dst=d["a"])
                   for j, (d, s) in enumerate(pairs)]
-            e.remote_dma_fused(tr, local_sem=T.sem["rl%d" % k])
+            e.remote_dma_fused(tr, local_sem=T.sem["rl%d" % loc])
+        loc = nrem[1]
+        nrem[1] += 1
         by = sum(s["cnt"] * s["sz"] * 128 for d, s in pairs)
         me = add("pool", "r", emit, [s for d, s in pairs], [d for d, s in pairs], 1000.0, 2500 + by / 70.0)
-        ops[me]["rem"] = (k, per * len(pairs))
+        ops[me].update(rem=(k, per * len(pairs)), loc=loc, eng_t=by / 140.0)
+
+    nland = [0, 0]
+
+    def bounce(hi_, alu, items, relay=()):
+        k = nrem[0]
+        nrem[0] += 1 + (len(relay) > 0)
+        helper = mates[hi_]
+        w = items[0][1][0]["cnt"]
+        home = [x[0] for x in items if x[0] is not None]
+        land = []
+        for x in items:
+            if nland[hi_] % 4096 + w > 4096:
+                nland[hi_] += 4096 - nland[hi_] % 4096
+            a = nland[hi_] % 16384
+            land.append(c2(("LO0", "LO1", "HI0", "HI1")[a // 4096], a % 4096, a % 4096 + w))
+            nland[hi_] += w
+
+        def masks(eng, m):
+            per = 1
+            while 2 * per * m <= len(eng):
+                per *= 2
+            return per, [sum(1 << x for x in eng[j * per:(j + 1) * per]) for j in range(m)]
+
+        def dst(c):
+            return [DstId(rid=topo.addr(c)[0], pnc=topo.addr(c)[1])]
+        pin, out = masks(topo.engines(core, helper), len(items))
+        far = topo.engines(helper, down) if hi_ == 0 else []
+        pbk, back = masks([e for e in topo.engines(helper, core) if e not in far], len(items))
+        pfr, on = masks(far, len(relay)) if relay else (0, [])
+
+        def emit(e):
+            e.remote_dma_fused([RemoteDMATransfer(dst_ids=dst(helper), dma_engine_mask=m, remote_sem=T.sem["rr%d" % k],
+                                                  srcs=[s["a"] for s in x[1]], dsts=[z["a"]], alu_op=alu if len(x[1]) > 1 else 0)
+                                for m, x, z in zip(out, items, land)], local_sem=T.sem["bl" if home else "rr%d" % k])
+
+        def hand_on(e):
+            e.wait_ge(T.sem["rr%d" % k], pin * len(items))
+            tr = [RemoteDMATransfer(dst_ids=dst(core), dma_engine_mask=m, remote_sem=T.sem["rr%d" % k], src=z["a"], dst=x[0]["a"])
+                  for m, x, z in zip(back, items, land) if home]
+            tr += [RemoteDMATransfer(dst_ids=dst(down), dma_engine_mask=m, remote_sem=T.sem["rr%d" % (k + 1)],
+                                     src=land[j]["a"], dst=z["a"]) for m, (z, j) in zip(on, relay)]
+            e.remote_dma_fused(tr, local_sem=T.sem["bl"])
+            return pbk * len(home) + pfr * len(relay)
+        srcs = [s for x in items for s in x[1]]
+        mine = sum(s["cnt"] * 512 for s in srcs) / 500.0
+        there = [dict(z, n="%d%s" % (hi_, z["n"])) for z in land]
+        me = add("pool", "b", emit, srcs, home + there, 1000.0,
+                 5000 + mine + w * 512 * len(home) / 300.0, [z for z, j in relay])
+        ops[me].update(rem=(k, (pbk if home else pin) * len(items), pfr * len(relay), pin * len(home)),
+                       helper=(hi_, hand_on), eng_t=mine, far=w * 512 * len(relay) / 70.0)
 
     def credit(regions):
         k = nrem[0]
         nrem[0] += 1
         rid, pid = topo.addr(up)[0], topo.addr(up)[1]
         m = 1 << topo.engines(core, up)[0]
-        me = add("pool", "r", lambda e: e.remote_sem_update(T.sem["rr%d" % k], T.sem["rl%d" % k], pid, rid, m),
+        loc = nrem[1]
+        nrem[1] += 1
+        me = add("pool", "r", lambda e: e.remote_sem_update(T.sem["rr%d" % k], T.sem["rl%d" % loc], pid, rid, m),
                  [], regions, 800.0, 2500.0)
-        ops[me]["rem"] = (k, 1)
+        ops[me].update(rem=(k, 1), loc=loc)
 
-    def shift(name, a, w):
-        dma(ap(name, slice(0, 112), slice(3072 + a, 3072 + a + w)), ap(name, slice(16, 128), slice(a, a + w)))
-        dma(ap(name, slice(112, 128), slice(3072 + a, 3072 + a + w)), ap(name, slice(0, 16), slice(a, a + w)))
+    def shift(name, a, w, src=None, s=None):
+        src, s = (name, a) if src is None else (src, s)
+        dma(c2(name, 3072 + a, 3072 + a + w, part=slice(0, 112)), c2(src, s, s + w, part=slice(16, 128)))
+        dma(c2(name, 3072 + a, 3072 + a + w, part=slice(112, 128)), c2(src, s, s + w, part=slice(0, 16)))
 
     def publish(names, a, w):
         send([(c2(x, 2048 + a, 2048 + a + w), c2(x, a, a + w)) for x in names])
         for x in names:
             shift(x, a, w)
 
-    idb, idn, idf, idh = ap("IDB"), ap("IDN"), ap("IDF"), ap("IDH")
+    p1, n1, nh, w12, w20 = [ap(x) for x in ("P1", "N1", "NH", "W12", "W20")]
+    idf, idn, id4, id8 = ap("IDF"), ap("IDN"), ap("ID4"), ap("ID8")
 
     dma(c2("IN1", 0, 1024), c2("th", 0, 1024))
     dma(c2("IN1", 1024, 2048), c2("dl", 0, 1024))
@@ -223,440 +309,620 @@ def build(g, core, T, topo):
     dma(c2("IN1", 3072, 4096), c2("dl", 1024, 2048))
     dma(ap("SLI"), ap("sl"))
     dma(ap("RFI"), ap("rf"))
-    dma(ap("FS"), ap("dr"))
-    ts(idb, ap("XD"), 0.0, None, A.is_equal)
-    ts(idn, ap("XD"), 0.0, -1.0, A.is_equal, A.mult)
-    ts(idf, ap("XD"), 0.0, None, A.is_equal)
-    ts(idh, ap("XD"), 0.0, 0.5, A.is_equal, A.mult)
+    dma(ap("LE0"), ap("dr"))
+    for w, x in ((p1, 1.0), (n1, -1.0), (nh, -0.5), (w12, -4096.0), (w20, 2.0 ** 20), (idf, 1.0), (idn, -1.0), (id4, 4.0), (id8, 8.0)):
+        ts(w, ap("XD"), 0.0, x, A.is_equal, A.mult)
     iota(c2("PC", 0, 1), [[0, 1]], 0, 1)
     iota(ap("XI"), [[1, 144]], -16, 0)
-    iota(c2("OK", 0, 256), [[0, 4], [1024, 2], [16, 32]], 0, 0)
-    iota(ap("CJ"), [[-4096, 4], [0, 16]], 12288, 0)
+    iota(ap("VI"), [[0, 4], [1024, 2], [16, 32]], 0, 0)
+    iota(ap("CJ"), [[0, 2], [-4096, 4], [0, 16]], 16384, 0)
     ts(c2("PC", 1, 2), c2("PC", 0, 1), 112, None, A.bitwise_and)
     ts(c2("PC", 2, 3), c2("PC", 0, 1), 15, None, A.bitwise_and)
     ts(c2("PC", 3, 4), c2("PC", 2, 3), 1, None, A.arith_shift_right)
-    cp(c2("PF", 0, 4), c2("PC", 0, 4))
+    ts(c2("PC", 4, 5), c2("PC", 0, 1), 4, 1, A.arith_shift_right, A.bitwise_and)
+    cp(c2("PF", 0, 5), c2("PC", 0, 5))
     g16, pm, ph = c2("PF", 1, 2), c2("PF", 2, 3), c2("PF", 3, 4)
-    ts(c2("PF", 16, 32), c2("XI", 16, 32), pm, None, A.is_equal)
+    ts(c2("PF", 16, 18), c2("XI", 16, 18), c2("PF", 4, 5), None, A.is_equal)
+    for s in range(2):
+        for e in range(2):
+            ts(c2("WS", 128 * (2 * s + e), 128 * (2 * s + e) + 128), ap("XD"), 16.0 * (e - s), c2("PF", 16 + s, 17 + s),
+               A.is_equal, A.mult)
+    add("dve", "c", lambda e: [e.memset(T["XT"][:], 0.0)], [], [ap("XT")], 50 + 512 * CY)
     ts(c2("PF", 8, 16), c2("XI", 16, 24), ph, None, A.is_equal)
-    ts(c2("PF", 5, 6), pm, 8.0, 2048.0, A.is_equal, A.mult)
-    for a, w in ((0, 8192.0), (144, 16384.0)):
-        ts(c2("UP", a, a + 144), ap("XI"), g16, w, A.is_equal, A.mult)
-        ts(c2("UN", a, a + 144), ap("XI"), g16, -w, A.is_equal, A.mult)
+    ts(c2("UP", 0, 144), ap("XI"), g16, 16384.0, A.is_equal, A.mult)
+    ts(c2("UP", 144, 288), ap("XI"), g16, 32768.0, A.is_equal, A.mult)
+    ts(c2("UN", 0, 144), ap("XI"), g16, -32768.0, A.is_equal, A.mult)
+    ts(c2("UN", 144, 288), ap("XI"), g16, -16384.0, A.is_equal, A.mult)
     for j in range(5):
         ts(c2("YM", 144 * j, 144 * j + 144), ap("XI"), g16, c2("PF", 8 + j, 9 + j), A.is_equal, A.mult)
-    for r in range(16):
-        ts(c2("ZM", 144 * r, 144 * r + 144), ap("XI"), g16, c2("PF", 16 + r, 17 + r), A.is_equal, A.mult)
-    ts(ap("VC0"), ap("OK"), pm, None, A.add)
+    ts(ap("VC0"), ap("VI"), pm, -MID, A.add, A.add)
     ts(ap("VC1"), ap("VC0"), 512.0, None, A.add)
-    ts(c2("RT", 2048, 2064), c2("XI", 0, 16), 0.0, c2("PF", 5, 6), A.mult, A.add)
+    ts(c2("CM", 0, 256), ap("VI"), 0.0, 1.0 / 128, A.mult, A.add)
+    ts(c2("PF", 19, 20), c2("PF", 12, 13), -1.0, 1.0, A.mult, A.add)
     for par in range(2):
         for kk in range(2):
-            cp(ap("SP%d" % par, slice(None), slice(0, 4), kk), ap("SLI", slice(None), par + 2 * kk))
-        cp(ap("SP%d" % par, slice(None), 4), ap("RFI", slice(None), slice(None), par))
-        for kk in range(2):
-            cp(c2("SU%d" % par, 128 * kk, 128 * kk + 128), ap("SLI", slice(None), par + 2 * kk))
+            cp(ap("SP%d" % par, al, al, kk), ap("SLI", al, par + 2 * kk))
+        cp(ap("SU%d" % par), ap("SP%d" % par))
+    ts(ap("RR"), ap("RFI"), -MID, None, A.add)
 
     bank = [("KA", 0), ("KA", 512), ("KA", 1024), ("KB", 0), ("KB", 512), ("KB", 1024)]
     nb = [0]
 
     def ends(src, dst0):
         for a in (0, 512):
-            for tab, sg in (("LO0", idn), ("HI0", idb)):
+            for tab, sg in (("LO0", n1), ("HI0", p1)):
                 bn, bo = bank[nb[0] % 6]
                 nb[0] += 1
                 ps = c2(bn, bo, bo + 512)
-                mm([(ps, idb, c2("IN1", src + a, src + a + 512), True, False),
-                    (ps, sg, c2("IN1", src + 1024 + a, src + 1536 + a), False, True)])
+                group([(ps, p1, c2("IN1", src + a, src + a + 512)), (ps, sg, c2("IN1", src + 1024 + a, src + 1536 + a))])
                 if tab == "LO0":
-                    act(c2(tab, dst0 + a, dst0 + a + 512), ps, scale=0.0625)
+                    act(c2(tab, dst0 + a, dst0 + a + 512), ps, scale=-0.0625, bias=-5.0 / 256)
                 else:
-                    ts(c2(tab, dst0 + a, dst0 + a + 512), ps, 0.0625, None, A.mult)
+                    ts(c2(tab, dst0 + a, dst0 + a + 512), ps, 0.0625, 3.0 / 256, A.mult, A.add)
     ends(0, 0)
     shift("LO0", 0, 1024)
     shift("HI0", 0, 1024)
     ends(2048, 1024)
     ends(4096, 2048)
-    act(ap("FM"), ap("FS"), scale=0.0625, bias=-1.0 / 128)
-    act(ap("FS"), ap("FS"), scale=0.0625)
+    send([(c2("LE1", 0, 1024), c2("LE0", 0, 1024))])
+
+    def steps(a):
+        dr = c2("LE%d" % (a // 2048), a % 2048, a % 2048 + 1024)
+        act(c2("FS", a, a + 1024), dr, scale=0.0625)
+        act(c2("FM", a, a + 1024), dr, scale=-0.0625, bias=1.0 / 128)
+    steps(0)
+    steps(1024)
 
     def tables(par):
-        sp = ap("SP%d" % par)
-        ts(ap("DH"), sp, RND64, -RND64, A.add, A.add)
-        tt(ap("DL"), sp, ap("DH"), A.subtract)
-        for half in range(2):
-            for r in range(8 * half, 8 * half + 8):
-                o = c2("PI", r % 8, 512, 8)
-                mm([(o, c2("ZM", 144 * r + 16 - q, 144 * r + 144 - q),
-                     c2("DL" if q % 2 else "DH", 64 * (q // 2), 64 * (q // 2) + 64), q == 0, q == 9) for q in range(10)])
-            act(ap("SG", slice(None), slice(None), slice(8 * half, 8 * half + 8)), ap("PI"))
-        for kk in range(2):
-            a = 512 * (par + 2 * kk)
-            for x in ("ST", "RT"):
-                dma(c2(x, a, a + 512), ap("SG", slice(None), slice(32 * kk, 32 * kk + 32)))
+        srcs = [ap("SP%d" % par, al, j) for j in range(4)] + [ap("RR", al, al, par)]
+        for j, x in enumerate(srcs):
+            dh, dl = ap("XT", al, al, slice(2 * j, 32, 16)), ap("XT", al, al, slice(2 * j + 1, 32, 16))
+            act(dh, x)
+            tt(dl, x, dh, A.subtract)
+        xu = "XU%d" % par
+        add("dve", "c", lambda e: [e.transpose(T[xu][:], T["XT"][:])], [ap("XT")], [ap(xu)], 50 + 512 * CY)
 
-    def pick(out, j, w, extra=()):
-        it = [(out, c2("YM", 144 * j + 16 - r, 144 * j + 144 - r), c2("GB", r, 16 * w, 16), r == 0, r == 15 and not extra)
-              for r in range(16)]
-        mm(it + list(extra))
+    def tables_out(par):
+        a, xu = 512 * par, "XU%d" % par
+        for kk in range(2):
+            mm([(ap("PI", al, al, slice(16 * s, 16 * s + 16)), c2("WS", 128 * (2 * s + e), 128 * (2 * s + e) + 128),
+                 ap(xu, al, slice(16 * kk, 16 * kk + 16), slice(16 * e, 16 * e + 16)), e == 0, e == 1)
+                for s in range(2) for e in range(2)])
+            act(c2("ST", a + 1024 * kk, a + 1024 * kk + 512), ap("PI"))
+            if kk == 0:
+                publish(["ST"], a, 512)
+        if par == 0:
+            stop = c2("ST", 2048, 2049)
+            ts(stop, stop, c2("PF", 19, 20), c2("PF", 12, 13), A.mult, A.add)
+
+    def pick(out, j, w, g0):
+        return [(out, c2("YM", 144 * j + 16 - r, 144 * j + 144 - r), c2("GB", g0 + r, g0 + 16 * w, 16)) for r in range(16)]
+
+    def fetch(t, kk):
+        par = t % 2
+        lo, hi = "LO%d" % par, "HI%d" % par
+        a = 512 * (par + 2 * kk)
+        dma(ap("GH%d" % kk, al, al, 4), c2(hi, a, a + 512))
+        for h in range(2):
+            for m in range(2):
+                for j in range(4):
+                    o = 64 * j + 32 * kk + 16 * h
+                    mine = kk == 0 and h == 0 and (j >= 4 - OPT["vg0"] // 2 if t == 0 else m == 1 and j >= 4 - OPT["vg"])
+                    eng = "dve" if mine else "act"
+                    if m == 1:
+                        gather(eng, ap("GH%d" % kk, al, h, j), ap(hi), c2("SU%d" % par, o, o + 16))
+                    elif kk == 0 or h == 0:
+                        w = 16 + 16 * kk
+                        gather(eng, ap("GL%d" % kk, al, j, slice(256 * h, 256 * h + 16 * w)), ap(lo),
+                               c2("SU%d" % par, o, o + w), scale=-1.0, bias=-1.0 / 128)
 
     def chunk(t, k):
         par = t % 2
         kk, h = k // 2, k % 2
         c = 4 * t + k
-        lo, hi, nlo, nhi = "LO%d" % par, "HI%d" % par, "LO%d" % (1 - par), "HI%d" % (1 - par)
-        gl, gh, ind, ks = "GL%d" % (c % 4), "GH%d" % (c % 4), "IN%d" % (c % 2), "KA" if c % 2 == 0 else "KB"
-        kc, rb, zb, na = "KC%d" % (c % 2), "RB%d" % (c % 2), "ZB%d" % (c % 2), "NA%d" % (c % 2)
-        le, lt = "LE%d" % (c % 2), "LT%d" % (c % 2)
+        lo, nlo, nhi = "LO%d" % par, "LO%d" % (1 - par), "HI%d" % (1 - par)
+        gl, gh, ind, ks = "GL%d" % kk, "GH%d" % kk, "IN1", "KB"
+        rb, lt = ap("RB%d" % (c % 2)), "LT%d" % kk
         v0 = 512 * (par + 2 * kk) + 256 * h
 
-        def blk(name, i, w=1, base=0):
-            return c2(name, base + 256 * i, base + 256 * (i + w))
-        dma(blk(gl, 4), c2(lo, v0, v0 + 256))
-        dma(blk(gh, 4), c2(hi, v0, v0 + 256))
-        for tab, dst in ((lo, gl), (hi, gh)):
-            for j in range(4):
-                o = 32 * j + 128 * kk + 16 * h
-                mine = k == 0 and j >= OPT["g0"] and (tab == hi or t == 0)
-                gather("dve" if mine else "act", blk(dst, j), ap(tab), c2("SU%d" % par, o, o + 16))
-        kq = ks
-        if OPT["sep"]:
-            kq, ks = "KA", "KB"
-        mn = blk(kq, 5)
-        for i, w in ((0, 2), (2, 2), (4, 1)):
-            if k == 0 and OPT["pe0"]:
-                mm([(blk(kq, i, w), idf, blk(gl, i, w), True, True)])
+        def key(i, w=1):
+            return c2(ks, 256 * i, 256 * (i + w))
+
+        def src(name, i, w=1):
+            if name[:2] in ("GH", "LT", "LE"):
+                return ap(name, al, h, slice(i, i + w))
+            return ap(name, al, slice(i, i + w), slice(256 * h, 256 * h + 256))
+
+        def bit(s, i, w=1):
+            o = 1280 * (s + 2 if s > 1 else s + 2 * (c % 2)) + 256 * i
+            return c2(ind, o, o + 256 * w)
+
+        def low_(i, w=1):
+            return c2("KA", 256 * i, 256 * (i + w))
+
+        for i in (0, 2):
+            if k in OPT["pelo"]:
+                group([(low_(i, 2), idf, src(gl, i, 2))])
             else:
-                act(blk(kq, i, w), blk(gl, i, w))
-        cuts = (0, 2, 4, 5) if k in OPT["split"] else OPT["cuts"]
-        for a, b in zip(cuts[:-1], cuts[1:]):
-            for s, (rot, src) in enumerate(((1, gl), (2, gl), (1, gh), (2, gh), (3, gh), (4, gh))):
-                for x, y, wrap in ((a, min(b, 5 - rot), False), (max(a, 5 - rot), b, True)):
+                act(low_(i, 2), src(gl, i, 2))
+        own = c2(lo, v0, v0 + 256)
+        act(low_(4), own, scale=-1.0, bias=-1.0 / 128)
+        tt(bit(0, 1, 4), low_(1, 4), src(gl, 0, 4), A.is_ge)
+        tt(bit(0, 0), low_(4), src(gl, 0), A.is_lt)
+        tt(bit(1, 2, 3), low_(2, 3), src(gl, 0, 3), A.is_ge)
+        tt(bit(1, 0, 2), low_(3, 2), src(gl, 0, 2), A.is_lt)
+        for a, b in OPT["cuts"][k]:
+            for rot in range(1, 5):
+                for x, y in ((a, min(b, 5 - rot)), (max(a, 5 - rot), b)):
                     if y > x:
-                        op = A.is_ge if (wrap and src == gl) else A.is_gt
-                        tt(blk(ind, x, y - x, 1280 * s), blk(kq, x, y - x), blk(src, (x + rot) % 5, y - x), op)
-        back = {0: [(0, 1, 4, 0), (1, 1, 0, 0), (0, 2, 3, 1)], 2: [(2, 2, 1, 0), (2, 2, 0, 1)], 4: [(4, 1, 3, 0), (4, 1, 2, 1)]}
-        pre = OPT["presum"] and k not in OPT["short"]
-        if pre:
-            dma(c2(ind, 2560, 3840), c2(ind, 3840, 5120), accum=True)
-            dma(c2(ind, 5120, 6400), c2(ind, 6400, 7680), accum=True)
+                        tt(bit(1 + rot, x, y - x), low_(x, y - x), src(gh, (x + rot) % 5, y - x), A.is_gt)
+        back = {0: [(0, 2, 0, 1), (0, 2, 1, 2)], 2: [(2, 2, 0, 3), (2, 1, 1, 4), (3, 1, 1, 0)], 4: [(4, 1, 0, 0), (4, 1, 1, 1)]}
         for i, w in ((0, 2), (2, 2), (4, 1)):
-            fw = ([(blk(ks, i, w), idf, blk(gl, i, w), True, False)]
-                  + [(blk(ks, i, w), idb if s < 2 else idn, blk(ind, i, w, 1280 * s), False, False)
-                     for s in ((0, 1, 2, 4) if pre else range(6))])
-            bw = [(blk(ks, x, ww), idn, blk(ind, y, ww, 1280 * s), False, (x, ww, y, s) == back[i][-1])
-                  for x, ww, y, s in back[i]]
+            parts = [[(key(i, w), idf, src(gl, i, w)) if i < 4 else (key(4), idn, own)],
+                     [(key(i, w), p1, bit(s, i, w)) for s in range(2)] + [(key(x, ww), n1, bit(s, y, ww)) for x, ww, s, y in back[i]],
+                     [(key(i, w), n1, bit(s, i, w)) for s in range(2, 4)], [(key(i, w), n1, bit(s, i, w)) for s in range(4, 6)]]
             if i == 4:
-                mm(fw + bw)
-            elif OPT["sep"]:
-                mm(fw[:1])
-                mm(fw[1:4])
-                mm(fw[4:])
-                mm(bw)
+                group([x for p in parts for x in p] + [(key(4), n1, c2("CM", 0, 256))])
             else:
-                mm(fw)
-                mm(bw)
-        boost[0] = OPT["tail"][k]
-        act(ap(kc), blk(ks, 0, 2))
-        tt(ap(kc), blk(ks, 2, 2), ap(kc), A.max)
-        sp_ = blk(ks, 5)
-        tt(sp_, blk(ks, 4), blk(kc, 0), A.max)
-        tt(sp_, sp_, blk(kc, 1), A.max)
-        short = k in OPT["short"]
-        if short or not OPT["ract"]:
-            ts(ap(rb), sp_, RND1, -RND1, A.add, A.add)
-        else:
-            act(ap(rb), sp_, bias=RND1)
-            act(ap(rb), ap(rb), bias=-RND1)
-        newlo, newhi = c2(nlo, v0, v0 + 256), c2(nhi, v0, v0 + 256)
-        if short:
-            tt(sp_, sp_, ap(rb), A.subtract)
-            if t < 3:
-                act(newlo, sp_, bias=-1.0 / 128)
+                for m, p in enumerate(parts):
+                    mm([(o, l, r, m == 0, m == 3 and x == 1) for x, (o, l, r) in enumerate(p)])
+        kcn = "KC%d" % (c % 2)
+        kc, kd = c2(kcn, 0, 256), c2(kcn, 256, 512)
+
+        def chain(out, op):
+            if OPT["wide"]:
+                act(ap(kcn), key(0, 2))
+                tt(ap(kcn), key(2, 2), ap(kcn), op)
+                tt(key(5), key(4), kc, op)
+                tt(out, key(5), kd, op)
             else:
-                act(ap("AS"), sp_)
-            for j in range(5):
-                tt(blk(lt, j), sp_, blk(gh, j), A.is_gt)
-            dma(ap(gh), ap(lt), accum=True)
-            for j in range(4):
-                tt(blk(le, j), sp_, blk(gl, j), A.is_ge)
-            if OPT["sep"]:
-                act(mn, blk(gh, 0))
+                act(kc, key(0))
                 for j in range(1, 4):
-                    tt(mn, mn, blk(gh, j), A.min)
-                last = blk(gh, 4)
-            else:
-                act(blk(ks, 4, 2), blk(gh, 0, 2))
-                tt(blk(ks, 4, 2), blk(ks, 4, 2), blk(gh, 2, 2), A.min)
-                tt(ap(zb), blk(ks, 4), blk(gh, 4), A.min)
-                last = ap(zb)
-            if t < 3:
-                tt(newhi, mn, last, A.min)
-            else:
-                tt(mn, mn, last, A.min)
-                tt(ap(zb), mn, ap("AS"), A.add)
-                tt(ap(rb), mn, ap("AS"), A.subtract)
-                act(newlo, ap(zb), scale=8.0, bias=0.1875)
-                act(newhi, ap(rb), scale=8.0, bias=0.0625)
+                    tt(kc, key(j), kc, op)
+                tt(out, key(4), kc, op)
+        top = key(5)
+        boost[0] = OPT["end"] if c == 15 else OPT["edge"] if k == 3 else 0.0
+        chain(top, A.max)
+        if k in OPT["vround"]:
+            ts(rb, top, RND1, -RND1, A.add, A.add)
         else:
-            tt(blk(na, 0), ap(rb), sp_, A.subtract)
-            if OPT["nadma"]:
-                for j in range(1, 5):
-                    dma(blk(na, j), blk(na, 0))
-            else:
-                acts([(blk(na, j), blk(na, 0)) for j in range(1, 5)])
-            dma(ap(gh), ap(na), accum=True)
-            dma(blk(gl, 0, 4), blk(na, 0, 4), accum=True)
+            act(rb, top, bias=RND1)
+            act(rb, rb, bias=-RND1)
+        newlo, newhi = c2(nlo, v0, v0 + 256), c2(nhi, v0, v0 + 256)
+        low, na = c2("AS", 256 * h, 256 * h + 256), c2("NA%d" % kk, 256 * h, 256 * h + 256)
+        if kind(t, k) == "P":
+            for i in (0, 2):
+                mm([(key(i, 2), idf, src(gh, i, 2), True, False)])
+        tt(top, top, rb, A.subtract)
+        if t < 3:
+            act(newlo, top, scale=-1.0)
+        else:
+            act(low, top)
+            act(na, low, scale=-1.0, bias=1.0 / 128)
+        if kind(t, k) == "D":
+            act(na, newlo, bias=1.0)
+            for j in range(5):
+                dma(c2("N5", 256 * j, 256 * j + 256), na)
+            dma(src(gh, 0, 5), ap("N5"), accum=True)
+            for x, y in ((0, 3), (3, 2)):
+                act(src(lt, x, y), src(gh, x, y), scale=-1.0, bias=1.0 - 2.0 ** -21, func=AF.Sign)
+        for j in range(0 if kind(t, k) == "D" else 5):
+            tt(src(lt, j), top, src(gh, j), A.is_gt)
+        keep, boost[0] = boost[0], 0.0
+        if (t, k) in OPT["vle"]:
+            for j in range(4):
+                tt(src("LE%d" % kk, j), top, src(gl, j), A.is_ge)
+        if kind(t, k) == "P":
+            boost[0] = keep
+            for i in (0, 2):
+                mm([(key(i, 2), p1, src(lt, i, 2), False, True)])
+            group([(key(4), idf, src(gh, 4)), (key(4), p1, src(lt, 4))])
+            mn = newhi if t < 3 else low_(5)
+            chain(mn, A.min)
+            if t == 3:
+                tt(newlo, mn, low, A.add)
+                tt(newhi, mn, na, A.add)
+            boost[0] = 0.0
+            return
+        dma(src(gh, 0, 5), src(lt, 0, 5), accum=True)
+        if kind(t, k) == "F":
+            waiting.append((newlo, newhi, low, na, ap("OL%d" % h), [ap(gh, al, h, j) for j in range(5)],
+                            [c2(x, 2048 + v0, 2304 + v0) for x in (nlo, nhi)]))
+            if OPT["pair"] and k == 0:
+                return
+            far = range(len(waiting) if kk == 0 else 0)
             if t < 3:
-                act(newlo, blk(na, 0), scale=-1.0, bias=-1.0 / 128)
-                act(newhi, blk(na, 0), scale=-1.0, bias=1.0)
+                bounce(0, 3, [(x[1], x[5]) for x in waiting], [(waiting[m][6][1], m) for m in far])
             else:
-                act(newlo, blk(na, 0), scale=-16.0, bias=0.125)
-            act(ap(lt), ap(gh), scale=-1.0, bias=-2.0 ** -21, func=AF.Sign)
-            dma(ap(gh), ap(lt), accum=True)
-            act(ap(le), blk(gl, 0, 4), scale=-1.0, bias=2.0 ** -21, func=AF.Sign)
-            act(mn, blk(gh, 0))
-            for j in range(1, 4):
-                tt(mn, mn, blk(gh, j), A.min)
-            tt(ap(zb), mn, blk(gh, 4), A.min)
-            if t < 3:
-                dma(newhi, ap(zb), accum=True)
-            else:
-                act(newhi, ap(zb), scale=8.0, bias=8.0625)
-                dma(newlo, newhi, accum=True)
-        boost[0] = 0.0
-        o = c2("PL", 64 * k, 64 * k + 64)
-        u0 = 144 if short else 0
-        it = []
-        for r in range(16):
-            it.append((o, c2("UP", u0 + 16 - r, u0 + 144 - r), c2(le, r, 1024, 16), r == 0, False))
-            it.append((o, c2("UN", u0 + 16 - r, u0 + 144 - r), c2(lt, r, 1024, 16), False, False))
-        it.append((o, idb, ap("CJ"), False, False))
-        it.append((o, idf, ap("SP%d" % par, slice(None), slice(0, 4), kk, slice(16 * h, 16 * h + 16)), False, True))
-        mm(it)
-        act(ap("KS%d" % par, slice(None), slice(None), kk, slice(16 * h, 16 * h + 16)), o)
+                bounce(0, 3, [(x[4], x[5]) for x in waiting])
+                bounce(0, 1, [(x[e], [x[4], x[2 + e]]) for x in waiting for e in range(2)],
+                       [(waiting[m][6][e], 2 * m + e) for m in far for e in range(2)])
+            del waiting[:]
+            return
+        top = low_(5)
+        act(top, src(gh, 0))
+        for j in range(1, 4):
+            tt(top, top, src(gh, j), A.min)
+        if kind(t, k) == "D":
+            tt(top, top, src(gh, 4), A.min)
+            tt(newhi, top, newlo, A.subtract)
+        elif t < 3:
+            tt(newhi, top, src(gh, 4), A.min)
+        else:
+            tt(top, top, src(gh, 4), A.min)
+            tt(newlo, top, low, A.add)
+            tt(newhi, top, na, A.add)
+
+    waiting = []
+
+    def kind(t, k):
+        return OPT["kinds"][t][k]
+
+    def holds(t, kk):
+        par = t % 2
+        gl, le, lt = "GL%d" % kk, "LE%d" % kk, "LT%d" % kk
+        byv = [(t, 2 * kk + h) in OPT["vle"] for h in range(2)]
+        sgn = [kind(t, 2 * kk + h) == "D" for h in range(2)]
+        halves = ((0, 2),) if byv[0] == byv[1] and sgn[0] == sgn[1] else ((0, 1), (1, 1))
+        for h0, hn in ((0, 2),) if byv[0] == byv[1] else halves:
+            q = slice(256 * h0, 256 * (h0 + hn))
+            a = 512 * (par + 2 * kk) + 256 * h0
+            na = c2("LO%d" % (1 - par), a, a + 256 * hn) if t < 3 else ap("NA%d" % kk, al, q)
+            m = OPT["many"]
+            for j in range(0 if byv[h0] or m == 1 else m):
+                dma(ap("N4", al, j, q), na)
+            for j in range(0 if byv[h0] else 4):
+                if j % m == 0:
+                    dma(ap(gl, al, slice(j, j + m), q), na if m == 1 else ap("N4", al, slice(0, m), q), accum=True)
+                act(ap(le, al, slice(h0, h0 + hn), j), ap(gl, al, j, q), scale=-1.0,
+                    bias=2.0 ** -21 + (1.0 / 128 if t == 3 else 0.0), func=AF.Sign)
+        for h0, hn in halves:
+            o = c2("PL", 128 * kk + 64 * h0, 128 * kk + 64 * (h0 + hn))
+            part = [(c2("PL", 128 * kk + 64 * h, 128 * kk + 64 * h + 64), slice(16 * h, 16 * h + 16)) for h in range(h0, h0 + hn)]
+            un, up_ = 144 * sgn[h0], 144 * byv[h0]
+            bias = -294912.0 - 262144.0 * sgn[h0] + 262144.0 * (not byv[h0])
+
+            def col(name, r):
+                return ap(name, al, slice(h0, h0 + hn), slice(0, 4), slice(r, 256, 16))
+            group([(o, c2("UN", un + 16 - r, un + 144 - r), col(lt, r)) for r in range(16)]
+                  + [(o, p1, c2("CJ", 0, 64 * hn))] + [(x, idf, ap("SP%d" % par, al, al, kk, q)) for x, q in part]
+                  + [(o, c2("UP", up_ + 16 - r, up_ + 144 - r), col(le, r)) for r in range(16)])
+            for x, q in part:
+                act(ap("KS%d" % par, al, al, kk, q), x, bias=bias - MID)
+        if t == 3:
+            elect(3, slice(kk, kk + 1), slice(0, 32))
 
     def drift(t):
         par = t % 2
         lo, hi, nlo, nhi = "LO%d" % par, "HI%d" % par, "LO%d" % (1 - par), "HI%d" % (1 - par)
-        for kk in range(2):
-            a = 512 * (1 - par + 2 * kk)
-            if t < 3:
-                dma(c2(nlo, a, a + 512), c2(lo, a, a + 512))
-                dma(c2(nhi, a, a + 512), c2(hi, a, a + 512))
-                dma(c2(nlo, a, a + 512), c2("FM", a, a + 512), accum=True)
-                dma(c2(nhi, a, a + 512), c2("FS", a, a + 512), accum=True)
-            else:
-                tmp = c2("TMP", 512 * kk, 512 * kk + 512)
-                act(c2(nlo, a, a + 512), c2(lo, a, a + 512), scale=8.0, bias=0.1875)
-                act(c2(nhi, a, a + 512), c2(lo, a, a + 512), scale=-8.0, bias=0.0625)
-                act(tmp, c2(hi, a, a + 512), scale=8.0)
-                dma(c2(nlo, a, a + 512), tmp, accum=True)
-                dma(c2(nhi, a, a + 512), tmp, accum=True)
-                dma(c2(nlo, a, a + 512), c2("dr", a, a + 512), accum=True)
-            if kk == 0:
-                publish([nlo, nhi], a, 512)
+        if t < 3:
+            items = [(c2(new, a, a + 512), [c2(old, a, a + 512), c2(step, a, a + 512)])
+                     for a in range(512 * (1 - par), 3072, 1024) for new, old, step in ((nlo, lo, "FM"), (nhi, hi, "FS"))]
+            for new, (old, step) in items[:OPT["here"]]:
+                dma(new, old)
+                dma(new, step, accum=True)
+            if items[OPT["here"]:]:
+                bounce(1, 1, items[OPT["here"]:])
+            for new in (nlo, nhi):
+                shift(new, 512 * (1 - par), 512)
+        elif OPT["here"] == 6:
+            for a in (0, 1024):
+                act(c2(nlo, a, a + 512), c2(lo, a, a + 512), scale=-1.0, bias=-1.0 / 128)
+                act(c2(nhi, a, a + 512), c2(lo, a, a + 512), bias=1.0 / 64)
+                for new, x in ((nhi, hi), (nlo, hi), (nlo, "FS"), (nlo, "FS")):
+                    dma(c2(new, a, a + 512), c2(x, a, a + 512), accum=True)
+            publish([nlo, nhi], 0, 512)
+        else:
+            items = []
+            for a in (0, 1024):
+                pos, neg = ap("YB%d" % (a // 1024)), c2("FM", a + 512, a + 1024)
+                act(pos, c2(lo, a, a + 512), scale=-1.0, bias=-1.0 / 128)
+                act(neg, c2(lo, a, a + 512), bias=1.0 / 64)
+                items += [(c2(nlo, a, a + 512), [pos] + [c2(x, a, a + 512) for x in (hi, "FS", "FS")]),
+                          (c2(nhi, a, a + 512), [neg, c2(hi, a, a + 512)])]
+            bounce(0, 1, items, [(c2(nlo, 2048, 2560), 0), (c2(nhi, 2048, 2560), 1)])
+            for new in (nlo, nhi):
+                shift(new, 0, 512)
 
-    def elect(t, k0, nk):
+    def elect(t, q, cq):
         par = t % 2
-        spn, vc, ksn = "SP%d" % par, "VC%d" % par, "KS%d" % par
-        w, al, q = 32 * nk, slice(None), slice(k0, k0 + nk)
-        boost[0] = OPT["boost"]
+        spn, ksn = "SP%d" % par, "KS%d" % par
+        w = (q.stop - q.start) * (cq.stop - cq.start)
+        boost[0] = OPT["boost"] * (OPT["last"] if t >= 2 else 1)
 
-        def sm(i):
-            return c2("SM", 64 * i, 64 * i + w)
-
-        def ix(i):
-            return c2("IX", 64 * i, 64 * i + w)
-        some, meet, take, d, kv, o1, o2, off, lim, nm = [sm(i) for i in range(10)]
-        rr, rows = ap(spn, al, 4, q), ap(spn, al, slice(0, 4), q)
-        kt, ca, gb = c2("KT", 0, w), c2("CA", 0, w), c2("GB", 0, 16 * w)
-        keep, new, ok, stay = c2("PI", 0, 4 * w), c2("PI", 256, 256 + 4 * w), c2("OK", 0, 4 * w), c2("STAY", 0, 4 * w)
-        tt(c2("M2", 0, 2 * w), ap(ksn, al, slice(0, 2), q), ap(ksn, al, slice(2, 4), q), A.max)
-        tt(kt, c2("M2", 0, w), c2("M2", w, 2 * w), A.max)
-        ts(ca, kt, 4095, None, A.bitwise_and)
-        ts(ix(0), ca, 2048.0, None, A.min)
-        ts(some, kt, float(THR), None, A.is_ge)
-        tt(c2("EQ", 0, w), ca, ap(vc, al, 0, q), A.is_equal)
-        ts(stay, ap(ksn, al, al, q), float(THR), None, A.is_ge)
-        tt(d, ca, rr, A.subtract)
+        def cut(name, i, m=1, base=0):
+            base += q.start * {"SB": 160, "M2": 64}.get(name, 128)
+            return c2(name, base + w * i, base + w * (i + m))
+        kt, d = [cut("SM", i) for i in range(2)]
+        take, o1, o2, top, ktp = [cut("SB", i) for i in range(5)]
+        tj = cut("TJ", 0, 4)
+        ix = [c2("IX", 64 * i + 32 * q.start, 64 * i + 32 * q.start + w) for i in range(4)]
+        g0 = 512 * q.start
+        rr, rows, ks = ap("RR", al, q, par, cq), ap(spn, al, al, q, cq), ap(ksn, al, al, q, cq)
+        gb, stay, nv, thr, ch = c2("GB", g0, g0 + 16 * w), cut("STAY", 0, 4), cut("NV", 0, 4), cut("THR", 0, 4), cut("CH", 0, 4)
+        tt(cut("M2", 0, 2), ap(ksn, al, slice(0, 2), q, cq), ap(ksn, al, slice(2, 4), q, cq), A.max)
+        tt(kt, cut("M2", 0), cut("M2", 1), A.max)
+        ts(top, kt, RND12, -RND12, A.add, A.add)
+        tt(cut("PL", 0, 1, 256), kt, top, A.subtract)
+        act(stay, ks, func=AF.Sign)
+        act(ktp, top, func=AF.Relu)
+        act(ch, ks, bias=RND12)
+        act(tj, ch, bias=-RND12)
         for m in range(3):
-            gather("act", gb, ap("RT"), ix(m))
-            hm = c2("PL", 256 + w * m, 256 + w * (m + 1))
-            pick(hm, 4, w)
-            if m < 2:
-                ts(ix(m + 1), hm, 2048.0, None, A.min)
-        tt(c2("EQ", w, 4 * w), c2("PL", 256, 256 + 3 * w), ap(vc, al, slice(1, 4), q), A.is_equal)
-        tt(c2("M2", 0, 2 * w), c2("EQ", 0, 2 * w), c2("EQ", 2 * w, 4 * w), A.max)
-        tt(meet, c2("M2", 0, w), c2("M2", w, 2 * w), A.max)
-        tt(take, some, meet, A.is_gt)
+            ts(ix[m], cut("PL", m, 1, 256), MID, 2048.0, A.add, A.min)
+            if m == 0:
+                tt(d, cut("PL", 0, 1, 256), rr, A.subtract)
+            gather("act", gb, c2("ST", 0, 2049), ix[m])
+            group(pick(cut("PL", m + 1, 1, 256), 4, w, g0))
+        tt(cut("EQ", 0, 4), cut("PL", 0, 4, 256), ap("VC%d" % par, al, al, q, cq), A.is_equal)
+        group([(cut("PI", 0), w20, cut("EQ", m)) for m in range(4)])
+        tt(take, cut("PI", 0), kt, A.is_lt)
         tt(d, d, take, A.mult)
         tt(rr, rr, d, A.add)
-        cp(ix(3), rr)
-        gather("act", gb, ap("ST"), ix(3))
+        ts(ix[3], rr, MID, None, A.add)
+        gather("act", gb, ap("ST"), ix[3])
         if t < 3:
             credit([c2("ST", 2048 + 512 * par, 2560 + 512 * par)])
-        ts(o1, rr, 2048.0, 2048.0, A.is_ge, A.mult)
-        ts(o2, rr, 3072.0, 1024.0, A.is_ge, A.mult)
-        tt(off, o1, o2, A.add)
-        act(nm, meet, scale=-1048576.0, bias=1048576.0)
-        tt(kv, kt, nm, A.add)
-        act(lim, o1, scale=-0.5, bias=4096.0)
-        tt(lim, lim, o2, A.add)
+        ts(o1, rr, 0.0, 2048.0, A.is_gt, A.mult)
+        ts(o2, rr, 1024.0, 1024.0, A.is_gt, A.mult)
+        group([(cut("PI", 0, 4, 256), n1, tj)] + [(cut("PI", j, 1, 256), l, r) for j in range(4) for l, r in ((p1, ktp), (w20, take))])
+        act(nv, cut("PI", 0, 4, 256), bias=-0.25, func=AF.Sign)
+        group([(cut("PI", 0, 4), w12, stay), (cut("PI", 0, 4), w12, nv)]
+              + [(cut("PI", j), l, r) for j in range(4) for l, r in ((nh, o1), (p1, o2))])
+        act(thr, cut("PI", 0, 4), bias=4096.0)
+        y = cut("PL", 0, 4, 256)
         for j in range(4):
-            tt(c2("PI", w * j, w * j + w), ap(ksn, al, j, q), kv, A.is_lt)
-        tt(keep, keep, stay, A.mult)
-        for j in range(4):
-            o = c2("PI", 256 + w * j, 256 + w * j + w)
-            pick(o, j, w, [(o, idf, off, False, True)])
-        for j in range(4):
-            tt(c2("OK", w * j, w * j + w), c2("PI", 256 + w * j, 256 + w * j + w), lim, A.is_lt)
-        tt(new, new, rows, A.subtract)
-        tt(ok, keep, ok, A.is_lt)
-        tt(new, new, ok, A.mult)
-        tt(rows, new, rows, A.add)
-        for kk in range(k0, k0 + nk):
-            cp(c2("SU%d" % par, 128 * kk, 128 * kk + 128), ap(spn, al, slice(0, 4), kk))
-        if t >= 2:
-            cp(ap("RF", al, q, par), rr)
+            o = cut("PL", j, 1, 256)
+            group([(o, p1, o1), (o, p1, o2)] + pick(o, j, w, g0))
+        tt(ch, y, thr, A.is_lt)
+        tt(y, y, rows, A.subtract)
+        tt(y, y, ch, A.mult)
+        tt(rows, y, rows, A.add)
+        if w == 64:
+            cp(ap("SU%d" % par), rows)
+        else:
+            for j in range(4):
+                o = 64 * j + 32 * q.start + cq.start
+                cp(c2("SU%d" % par, o, o + w), ap(spn, al, j, q.start, cq))
         if t < 3:
             tables(par)
-            publish(["ST"], 512 * par, 512)
+            tables_out(par)
         boost[0] = 0.0
 
-    tables(0)
-    tables(1)
-    publish(["ST"], 0, 1024)
+    for par in range(2):
+        tables(par)
     for t in range(4):
         par = t % 2
-        drift(t)
-        for k in range(4):
-            chunk(t, k)
-            if k == 1:
-                publish(["LO%d" % (1 - par)], 512 * par, 512)
-                publish(["HI%d" % (1 - par)], 512 * par, 512)
-                if t == 3:
-                    elect(3, 0, 1)
+        for kk in range(2):
+            fetch(t, kk)
+            if kk == 0:
+                if t == 0:
+                    gate[0] = len(ops) - 1
+                    steps(2048)
+                    for x in range(2):
+                        tables_out(x)
+                    gate[0] = None
+                boost[0] = OPT["early"]
+                drift(t)
+                boost[0] = 0.0
+            chunk(t, 2 * kk)
+            chunk(t, 2 * kk + 1)
+            if kk == 0:
+                for x in ("LO%d" % (1 - par), "HI%d" % (1 - par)):
+                    shift(x, 512 * par, 512)
+                    todo = [h for h in range(2) if kind(t, h) != "F" or (t < 3 and x[0] == "L")]
+                    if todo:
+                        a, b = 512 * par + 256 * todo[0], 512 * par + 256 * todo[-1] + 256
+                        if x[0] in OPT["relay"]:
+                            bounce(0, 0, [(None, [c2(x, a, b)])], [(c2(x, 2048 + a, 2048 + b), 0)])
+                        else:
+                            send([(c2(x, 2048 + a, 2048 + b), c2(x, a, b))])
+            holds(t, kk)
         if t < 3:
-            credit([c2("LO%d" % par, 2048, 3072), c2("HI%d" % par, 2048, 3072)])
-            elect(t, 0, 2)
-        else:
-            elect(3, 1, 1)
+            a, b = (2048, 3072) if t == 2 else (2560 - 512 * par, 3072 - 512 * par)
+            credit([c2("LO%d" % par, a, b), c2("HI%d" % par, a, b)])
+            elect(t, slice(0, 2), slice(0, 32))
 
-    dma(ap("yt"), c2("LO0", 0, 2048))
-    add("pe", "c", lambda e: [e.transpose(T["PI"][:, 0:128], T["RF"][:], T["IDF"][:])], [ap("RF"), idf],
+    for a in range(4):
+        act(c2("FM", 512 * a, 512 * a + 512), c2("LO0", 512 * a, 512 * a + 512), scale=8.0)
+        dma(c2("yt", 512 * a, 512 * a + 512), c2("FM", 512 * a, 512 * a + 512))
+    add("pe", "c", lambda e: [e.transpose(T["PI"][:, 0:4], T["RR"][:], T["IDF"][:])], [ap("RR"), idf],
         [c2("PI", 0, 128)], 300.0, 60)
-    act(ap("RFT"), c2("PI", 0, 128))
+    act(ap("RFT"), c2("PI", 0, 128), bias=MID)
     for gi in range(8):
         dma(ap("yr", gi), c2("RFT", 16 * gi, 16 * gi + 16))
-    for s, a in enumerate((0, 2, 1, 3)):
-        par, kk, zo = a % 2, a // 2, 2048 * (s % 2)
-        own = c2("FM", 512 * a, 512 * a + 512)
-        dma(own, c2("LO0", 512 * a, 512 * a + 512))
-        ps = c2("KA" if s % 2 == 0 else "KB", 0, 512)
-        mm([(ps, idh, c2("HI0", 512 * a, 512 * a + 512), True, False)])
+    for s, (a, x, w) in enumerate(((0, 0, 512), (2, 0, 512), (1, 0, 512), (3, 0, 256), (3, 256, 256))):
+        par, kk, zo, v0 = a % 2, a // 2, 2048 * (s % 2), 512 * a + x
+        own = c2("GL0", v0, v0 + w)
+        dma(own, c2("LO0", v0, v0 + w))
+        ps = c2("KA" if s % 2 == 0 else "KB", 512 * (s // 2), 512 * (s // 2) + w)
+        yb = c2("YB%d" % (s % 2), 0, w)
+        fold = s in OPT["fsum"]
+        terms = [c2("GL1", v0, v0 + w)]
+        if fold:
+            act(terms[0], c2("HI0", v0, v0 + w), scale=0.5)
+        else:
+            mm([(ps, id4, c2("HI0", v0, v0 + w), True, False)])
         for j in range(4):
-            off = c2("SU%d" % par, 32 * j + 128 * kk, 32 * j + 128 * kk + 32)
-            z = c2("LO1", zo + 512 * j, zo + 512 * j + 512)
-            p = c2("HI1", zo + 512 * j, zo + 512 * j + 512)
+            o = 64 * j + 32 * kk + x // 16
+            off = c2("SU%d" % par, o, o + w // 16)
+            z = c2("LO1", zo + 512 * j, zo + 512 * j + w)
+            p = c2("HI1", zo + 512 * j, zo + 512 * j + w)
             if j >= OPT["fin"][s]:
                 gather("act", z, ap("LO0"), off, scale=-1.0)
                 dma(z, own, accum=True)
-                act(z, z, scale=-1.0, func=AF.Sigmoid)
+                act(z, z, scale=-8.0, func=AF.Sigmoid)
             else:
                 gather("dve", z, ap("LO0"), off, other=own, op=A.subtract)
-                act(z, z, func=AF.Sigmoid)
+                act(z, z, scale=8.0, func=AF.Sigmoid)
+            if s == 0 and j == 0 and not lite:
+                ops[-1]["dur"] += 1300.0
+                first = len(ops) - 1
+            elif not lite:
+                ops[-1]["deps"].add((first, "R"))
             gather("dve", p, ap("HI0"), off, other=z, op=A.mult)
-            mm([(ps, idf, p, False, j == 3)])
-        act(ap("YB%d" % (s % 2)), ps)
-        dma(c2("yq", 512 * a, 512 * a + 512), ap("YB%d" % (s % 2)))
+            terms.append(p)
+            if not fold:
+                mm([(ps, id8, p, False, j == 3)])
+        if fold:
+            bounce(1, 1, [(yb, terms)])
+            act(yb, yb, scale=8.0)
+        else:
+            act(yb, ps)
+        dma(c2("yq", v0, v0 + w), yb)
     return ops
 
 
 def schedule(ops):
     n = len(ops)
-    real = ops
-    ops = [dict(o) for o in real]
-    for o in ops:
-        if o["kind"] == "d":
-            o["lat"] = 1800 + (o["lat"] - 1800) * OPT["ds"]
-            o["dur"] *= OPT["ds"]
-        elif o["kind"] == "r":
-            o["lat"] *= OPT["rs"]
-        elif o["eng"] == "pe":
-            o["dur"] *= OPT["ps"]
-        elif o.get("gat"):
-            o["dur"] *= OPT["gs"]
+    eng = [o["eng"] for o in ops]
+    banks = [sorted(o["banks"]) for o in ops]
+    pred = [sorted(set((d, w == "X") for d, w in o["deps"])) for o in ops]
     succ = [[] for _ in range(n)]
-    pred = [sorted(set(d for d, w in o["deps"])) for o in ops]
     for i in range(n):
-        for d in pred[i]:
-            succ[d].append(i)
+        for d, x in pred[i]:
+            succ[d].append((i, x))
 
-    def sweep(before, after, prio, back):
+    def costs(ds, rs, ls, cs, ss, ps, gs, hop):
+        dur, lat, use, far = [], [], [], []
+        for o in ops:
+            d, l, u = o["dur"], o["lat"], o.get("eng_t")
+            if o["kind"] == "d":
+                d, u = d * ds, (l - 1800) * ds
+                l = 1800 * (1 + ds) / 2 + u
+            elif o["kind"] == "b":
+                d, l, u = d * rs, l * rs, u * ds
+            elif o["kind"] == "r":
+                d, l, u = d * rs, 2500 * rs + (l - 2500) * ls, u and u * ls
+            else:
+                d *= {"dve": cs, "pe": ps, "act": ss}.get(o["eng"], 1) * (gs if o.get("gat") else 1)
+            dur.append(d)
+            lat.append(l)
+            use.append(u)
+            far.append(o.get("far", 0.0) * ls)
+        return dur, lat, use, far, hop
+
+    def sweep(cost, prio, back, look, beta):
+        dur, lat, use, far, hop = cost
+        before, after = (succ, pred) if back else (pred, succ)
         left = [len(p) for p in before]
-        free, bfree, blast, dfree = {}, {}, {}, 0.0
-        start, done = [0.0] * n, [0.0] * n
-        rdy = [o["lat"] if back else 0.0 for o in ops]
+        free, bfree, blast, dfree = {e: 0.0 for e in eng}, {}, {}, 0.0
+        done = [0.0] * n
+        rdy = list(lat) if back else [0.0] * n
         ready = set(i for i in range(n) if left[i] == 0)
         order, extra = [], []
         while ready:
             est = {}
             for i in ready:
-                o = ops[i]
-                s = max(rdy[i], free.get(o["eng"], 0.0))
-                for b in o["banks"]:
-                    if b in blast and ops[blast[b]]["eng"] != o["eng"]:
-                        s = max(s, bfree[b] + HOP)
+                s = max(rdy[i], free[eng[i]])
+                for b in banks[i]:
+                    if b in blast and eng[blast[b]] != eng[i] and bfree[b] + hop > s:
+                        s = bfree[b] + hop
                 est[i] = s
             first = min(ready, key=lambda i: (est[i], -prio[i], i))
-            e = ops[first]["eng"]
-            i = max((x for x in ready if ops[x]["eng"] == e and est[x] <= est[first] + OPT["look"]),
-                    key=lambda x: (prio[x], -x))
-            o = ops[i]
-            start[i] = est[i]
-            free[e] = est[i] + o["dur"]
-            done[i] = free[e] + (0.0 if back else o["lat"])
-            if o["kind"] == "d" and not back:
-                done[i] = max(done[i], dfree + o["lat"] - 1800)
-                dfree = done[i]
-            for b in o["banks"]:
-                if b in blast and ops[blast[b]]["eng"] != e:
+            e, t0 = eng[first], est[first]
+            i = max((x for x in ready if eng[x] == e and est[x] <= t0 + look),
+                    key=lambda x: (prio[x] - beta * (est[x] - t0), -x))
+            free[e] = est[i] + dur[i]
+            done[i] = free[e] + (0.0 if back else lat[i])
+            if use[i] and not back:
+                late = max(0.0, dfree - free[e] - 1800)
+                done[i] += late
+                dfree = free[e] + 1800 + late + use[i]
+            for b in banks[i]:
+                if b in blast and eng[blast[b]] != e:
                     extra.append((i, blast[b]))
                 blast[b] = i
                 bfree[b] = done[i]
             ready.discard(i)
             order.append(i)
-            for s in after[i]:
-                rdy[s] = max(rdy[s], done[i] + HOP + (ops[s]["lat"] if back else 0.0))
+            for s, x in after[i]:
+                rdy[s] = max(rdy[s], done[i] + hop + (lat[s] if back else 0.0) + (far[s if back else i] if x else 0.0))
                 left[s] -= 1
                 if left[s] == 0:
                     ready.add(s)
-        return order, start, done, extra
+        return order, done, extra
 
-    prio = [0.0] * n
-    for i in range(n - 1, -1, -1):
-        prio[i] = ops[i]["dur"] + ops[i]["lat"] + max([prio[s] + HOP for s in succ[i]] + [0.0])
-    base = list(prio)
-    prio = [p + o["boost"] for p, o in zip(prio, ops)]
+    def replay(cost, order, extra):
+        dur, lat, use, far, hop = cost
+        more = {}
+        for i, d in extra:
+            more.setdefault(i, []).append((d, False))
+        free, dfree, done = {e: 0.0 for e in eng}, 0.0, [0.0] * n
+        last, why, dlast = {}, [None] * n, None
+        for i in order:
+            s, why[i] = free[eng[i]], last.get(eng[i])
+            for d, x in pred[i] + more.get(i, []):
+                r = done[d] + hop + (far[d] if x else 0.0)
+                if r > s:
+                    s, why[i] = r, d
+            free[eng[i]] = s + dur[i]
+            last[eng[i]] = i
+            done[i] = s + dur[i] + lat[i]
+            if use[i]:
+                late = max(0.0, dfree - s - dur[i] - 1800)
+                if late > 0:
+                    why[i] = dlast
+                done[i] += late
+                dfree, dlast = s + dur[i] + 1800 + late + use[i], i
+        i, path = max(range(n), key=lambda x: done[x]), []
+        while i is not None:
+            path.append(i)
+            i = why[i]
+        return max(done), path
+
+    tests = [costs(*x) for x in SPEEDS]
     best = None
-    for turn in range(OPT["turns"]):
-        fw = sweep(pred, succ, prio, False)
-        if best is None or max(fw[2]) < max(best[2]):
-            best = fw
-        late = sweep(succ, pred, fw[2], True)[2]
-        prio = [OPT["mix"] * a + (1 - OPT["mix"]) * b for a, b in zip(late, prio if turn else base)]
-    return best
+    for plan, look, beta, cp in OPT["tries"]:
+        cost = costs(*plan)
+        prio = [0.0] * n
+        for i in range(n - 1, -1, -1):
+            prio[i] = cost[0][i] + cost[1][i] + max([prio[s] + cost[4] for s, x in succ[i]] + [0.0])
+        prio = [cp * p - (1 - cp) * prio[0] * i / n + ops[i]["boost"] for i, p in enumerate(prio)]
+        for turn in range(OPT["turns"]):
+            order, done, extra = sweep(cost, prio, False, look, beta)
+            spans = [replay(c, order, extra)[0] for c in tests]
+            score = sum(WEIGHTS[k] * x / (best[1] if best else spans)[k] for k, x in enumerate(spans))
+            if best is None or score < best[0]:
+                best = (score, best[1] if best else spans, order, done, extra, spans, (plan, look, beta, cp, turn), prio)
+            late = sweep(cost, done, True, look, beta)[1]
+            prio = [OPT["mix"] * (a + OPT["keep"] * o["boost"]) + (1 - OPT["mix"]) * b for a, b, o in zip(late, prio, ops)]
+    plan, look, beta = best[6][:3]
+    cost, prio = costs(*plan), list(best[7])
+    order, extra = best[2], best[4]
+    for turn in range(OPT["mend"]):
+        path = replay(tests[turn % len(tests)], order, extra)[1]
+        for i, d in zip(path, path[1:]):
+            if (d, False) not in pred[i] and (d, True) not in pred[i]:
+                prio[i] += OPT["step"]
+                prio[d] -= OPT["step"]
+            else:
+                prio[d] = max(prio[d], prio[i])
+        order, done, extra = sweep(cost, prio, False, look, beta)
+        spans = [replay(c, order, extra)[0] for c in tests]
+        score = sum(WEIGHTS[k] * x / best[1][k] for k, x in enumerate(spans))
+        if score < best[0]:
+            best = (score, best[1], order, done, extra, spans, (plan, look, beta, "mend", turn), list(prio))
+        elif turn % OPT["back"] == 0:
+            prio, order, extra = list(best[7]), best[2], best[4]
+    LAST["best"] = best[5:7]
+    return best[2], None, best[3], best[4]
 
 
 def rank_program(g, core, T, topo):
-    if T.rank_of(core) is None:
+    served = [(c, k) for c in T.cores for k, h in enumerate(neighbours(c, T, topo)) if h == core]
+    if T.rank_of(core) is None and not served:
         return
-    ops = build(g, core, T, topo)
     key = repr(sorted(OPT.items()))
+    ops = build(served[0][0] if served else core, T, topo, bool(served) and key in LAST)
     if key not in LAST:
         LAST[key] = schedule(ops)
     order, start, done, extra = LAST[key]
+    if served:
+        sent = sum(ops[i]["helper"][1](g) for i in order if ops[i].get("helper", (None,))[0] == served[0][1])
+        if sent:
+            g.wait_ge(T.sem["bl"], sent)
+        return
     for i, d in extra:
         ops[i]["deps"].add((d, "W"))
     LAST["plan"] = (ops, order, start, done)
@@ -693,9 +959,8 @@ def rank_program(g, core, T, topo):
             need(q, d, w, i)
         if o["kind"] == "c":
             sem = "e_" + q
-            for ins in o["emit"](queue[q]):
-                ins.then_inc(T.sem[sem], 1)
-                total[sem] = total.get(sem, 0) + 1
+            o["emit"](queue[q])[-1].then_inc(T.sem[sem], 1)
+            total[sem] = total.get(sem, 0) + 1
             o["tokR"] = o["tokW"] = (sem, total[sem], dict(known[q]))
         elif o["kind"] == "d":
             slot = [s for s in pools[q] if s[1] is None or [w for w in ops[s[1]]["waiters"] if w != i]][0]
@@ -712,12 +977,24 @@ def rank_program(g, core, T, topo):
             o["emit"](queue[q])[0].then_inc(T.sem[sem], 16)
             total[sem] = total.get(sem, 0) + 16
             o["tokR"] = o["tokW"] = (sem, total[sem], dict(known[q]))
+        elif o["kind"] == "b":
+            k, cnt, far, sent = o["rem"]
+            o["emit"](queue[q])
+            sem = "rr%d" % k
+            total[sem] = cnt
+            total["bl"] = total.get("bl", 0) + sent
+            when["bl"] = done[i]
+            o["tokR"] = o["tokW"] = (sem, cnt, dict(known[q]))
+            if far:
+                total["rr%d" % (k + 1)] = far
+                when["rr%d" % (k + 1)] = done[i]
+                o["tokX"] = ("rr%d" % (k + 1), far, {})
         else:
             k, cnt = o["rem"]
             o["emit"](queue[q])
-            total["rl%d" % k] = total["rr%d" % k] = cnt
+            sem = "rl%d" % o["loc"]
+            total[sem] = total["rr%d" % k] = cnt
             when["rr%d" % k] = done[i]
-            sem = "rl%d" % k
             o["tokR"] = (sem, cnt, dict(known[q]))
             o["tokW"] = ("rr%d" % k, cnt, {})
         when[sem] = done[i]

from concourse.bass import DstId, RemoteDMATransfer
from concourse.mybir import AluOpType, ActivationFunctionType

F, B, I, U = "float32", "bfloat16", "int32", "uint16"
NG, NS, NL, NR = 24, 47, 22, 52
SCRATCH = {
    "LO0": ("sbuf", [128, 4096], F), "LO1": ("sbuf", [128, 4096], F),
    "HI0": ("sbuf", [128, 4096], F), "HI1": ("sbuf", [128, 4096], F),
    "ST": ("sbuf", [128, 4096], B),
    "FM": ("sbuf", [128, 3072], F), "FS": ("sbuf", [128, 3072], F), "IN1": ("sbuf", [128, 10240], B), "AS": ("sbuf", [128, 512], F),
    "YM": ("sbuf", [128, 720], B), "UP": ("sbuf", [128, 288], B), "UN": ("sbuf", [128, 288], B),
    "SLI": ("sbuf", [128, 4, 4, 32], I), "RFI": ("sbuf", [128, 2, 2, 32], I), "RR": ("sbuf", [128, 2, 2, 32], F),
    "RFT": ("sbuf", [128, 128], F), "XI": ("sbuf", [128, 144], F), "XD": ("sbuf", [128, 128], F),
    "N1": ("sbuf", [128, 128], B), "NH": ("sbuf", [128, 128], B),
    "P1": ("sbuf", [128, 128], B), "W12": ("sbuf", [128, 128], B), "W20": ("sbuf", [128, 128], B),
    "IDF": ("sbuf", [128, 128], F), "IDN": ("sbuf", [128, 128], F), "ID4": ("sbuf", [128, 128], F), "ID8": ("sbuf", [128, 128], F),
    "PC": ("sbuf", [128, 8], I), "PF": ("sbuf", [128, 32], F), "VI": ("sbuf", [128, 256], F),
    "CJ": ("sbuf", [128, 128], B), "TJ": ("sbuf", [128, 256], B), "WS": ("sbuf", [128, 512], B),
    "XT": ("sbuf", [128, 32, 32], B), "XU0": ("sbuf", [128, 32, 32], B), "XU1": ("sbuf", [128, 32, 32], B), "M2": ("sbuf", [128, 128], F),
    "IX": ("sbuf", [128, 256], U), "SM": ("sbuf", [128, 320], F), "SB": ("sbuf", [128, 320], B),
    "CM": ("sbuf", [128, 256], B), "N4": ("sbuf", [128, 4, 512], F), "EQ": ("sbuf", [128, 256], B), "STAY": ("sbuf", [128, 256], B), "NV": ("sbuf", [128, 256], B),
    "THR": ("sbuf", [128, 256], F), "CH": ("sbuf", [128, 256], F),
    "GB": ("sbuf", [128, 1024], B),
    "KA": ("psum", [128, 1536], F), "KB": ("psum", [128, 1536], F),
    "PL": ("psum", [128, 512], F), "PI": ("psum", [128, 16, 32], F),
}
for _k in range(2):
    SCRATCH["GL%d" % _k] = ("sbuf", [128, 4, 512], F)
    SCRATCH["GH%d" % _k] = ("sbuf", [128, 2, 5, 256], F)
    SCRATCH["LE%d" % _k] = ("sbuf", [128, 2, 4, 256], B)
    SCRATCH["LT%d" % _k] = ("sbuf", [128, 2, 5, 256], B)
    SCRATCH["NA%d" % _k] = ("sbuf", [128, 512], F)
    SCRATCH["KC%d" % _k] = ("sbuf", [128, 512], F)
    SCRATCH["OL%d" % _k] = ("sbuf", [128, 256], F)
    SCRATCH["RB%d" % _k] = ("sbuf", [128, 256], F)
    SCRATCH["SP%d" % _k] = ("sbuf", [128, 4, 2, 32], F)
    SCRATCH["KS%d" % _k] = ("sbuf", [128, 4, 2, 32], F)
    SCRATCH["VC%d" % _k] = ("sbuf", [128, 4, 2, 32], F)
    SCRATCH["SU%d" % _k] = ("sbuf", [128, 256], U)
    SCRATCH["YB%d" % _k] = ("sbuf", [128, 512], F)
SEMAPHORES = (["e_pe", "e_dve", "e_act", "e_pool"] + ["dg%d" % k for k in range(NG)] + ["ds%d" % k for k in range(NS)]
              + ["bl"] + ["rl%d" % k for k in range(NL)] + ["rr%d" % k for k in range(NR)])

CY, PCY, GA, HOP = 0.92, 0.46, 1.56, 120.0
RND1 = 1.5 * 2.0 ** 23
RND12 = 1.5 * 2.0 ** 35
MID = 2047.5
SIZE = {F: 4, I: 4, B: 2, U: 2}
LAST = {}
SPEEDS = ((1, 1, 1, 0.87, 0.87, 0.87, 0.95, 60), (0.7, 1, 1, 1.25, 1.25, 1.25, 0.95, 60), (0.7, 1, 1, 1.05, 1.05, 1.05, 1.33, 60),
          (0.7, 1, 1, 0.87, 0.87, 1.3, 1, 60), (0.7, 2.2, 1, 0.87, 0.87, 0.87, 1, 200), (1.6, 1.2, 1, 0.87, 0.87, 0.87, 1, 60),
          (1, 1.3, 4, 0.87, 0.87, 0.87, 1, 100), (0.7, 1, 1, 0.87, 0.87, 0.87, 1, 400), (0.7, 1, 1, 0.87, 1.2, 0.87, 1, 60))
WEIGHTS = (1, 2, 2, 1, 2, 0.5, 0.5, 1.5, 1)
OPT = {"boost": 1500.0, "vg": 3, "vg0": 4, "fin": (2, 2, 2, 2, 4), "edge": 2000.0, "turns": 5, "mix": 0.6,
       "cuts": (((0, 2), (2, 5)),) * 4, "vround": (3,), "pelo": (), "kinds": ("FEEP", "FEEP", "FEEP", "EEEP"),
       "fsum": (), "pair": False, "end": 6000.0, "mend": 15, "step": 1000.0, "back": 10, "early": 20000.0, "last": 2.0,
       "tries": (((1.0, 2.0, 1.5, 1, 1.1, 1.15, 1.15, 150), 30.0, 0.0, 0.5),),
       "here": 6, "relay": "", "many": 2, "wide": False, "keep": 0.5, "vle": ((3, 2), (3, 3))}


def neighbours(core, T, topo):
    down = T.cores[(T.rank_of(core) - 1) % len(T.cores)]
    free = [c for c in topo.cores_of(core) if T.rank_of(c) is None and topo.die(c) == topo.die(core)]
    first = [c for c in free if topo.may_write(c, down)][0]
    return [first, [c for c in free if c != first][0]]


def build(core, T, topo, lite=False):
    A = AluOpType
    AF = ActivationFunctionType
    n = len(T.cores)
    rank = T.rank_of(core)
    down, up = T.cores[(rank - 1) % n], T.cores[(rank + 1) % n]
    mates = neighbours(core, T, topo)
    ops = []
    hist = {}
    boost, gate = [0.0], [None]
    al = slice(None)

    def ap(name, *idx):
        shape = list(T[name].shape)
        idx = list(idx) + [al] * (len(shape) - len(idx))
        runs, cnt, stride, pr, full = [(0, 1)], 1, 1, None, True
        for d in range(len(shape) - 1, -1, -1):
            x = idx[d]
            r = range(x, x + 1) if isinstance(x, int) else range(*x.indices(shape[d]))
            if d == 0:
                pr = (r[0], r[-1] + 1)
                break
            cnt *= len(r)
            if len(runs) == 1 and runs[0] == (0, stride) and r.step == 1:
                runs = [(r[0] * stride, (r[-1] + 1) * stride)]
            elif len(runs) * len(r) <= 8:
                runs = [(a + i * stride, b + i * stride) for i in r for a, b in runs]
            else:
                runs, full = [(runs[0][0] + r[0] * stride, runs[-1][1] + r[-1] * stride)], False
            stride *= shape[d]
        where, dtype = (SCRATCH[name][0], SCRATCH[name][2]) if name in SCRATCH else ("dram", F)
        return {"a": T[name][tuple(idx)], "n": name, "p": pr, "runs": runs, "full": full, "cnt": cnt,
                "ps": where == "psum", "sz": SIZE[dtype]}

    def c2(name, a, b, step=1, part=al):
        shape, idx = list(T[name].shape)[1:], [part]
        for d in range(len(shape)):
            inner = 1
            for x in shape[d + 1:]:
                inner *= x
            if d == len(shape) - 1:
                idx.append(slice(a, b, step))
            elif a // inner == (b - 1) // inner:
                idx.append(a // inner)
                a, b = a % inner, (b - 1) % inner + 1
            else:
                idx.append(slice(a // inner, b // inner))
                break
        return ap(name, *idx)

    def add(eng, kind, emit, R, W, dur, lat=0.0, X=()):
        me = len(ops)
        deps = set()
        if lite:
            ops.append({})
            return me
        if gate[0] is not None:
            deps.add((gate[0], "W"))
        for acc, wr in [(x, "") for x in R] + [(x, "W") for x in W] + [(x, "X") for x in X]:
            h = hist.setdefault(acc["n"], [])
            for e in h:
                if e[4] != me and e[0] < acc["p"][1] and acc["p"][0] < e[1] and (e[5] or wr):
                    if [1 for a, b in acc["runs"] if e[2] < b and a < e[3]]:
                        deps.add((e[4], e[5] or "R"))
            if wr and acc["full"]:
                h[:] = [e for e in h if not (acc["p"][0] <= e[0] and e[1] <= acc["p"][1]
                                             and [1 for a, b in acc["runs"] if a <= e[2] and e[3] <= b])]
            h.extend((acc["p"][0], acc["p"][1], a, b, me, wr) for a, b in acc["runs"])
        banks = set()
        for acc in R + W:
            if acc["ps"]:
                for a, b in acc["runs"]:
                    for x in range(a // 512, (b - 1) // 512 + 1):
                        banks.add((acc["n"], x))
        ops.append({"eng": eng, "kind": kind, "emit": emit, "deps": deps, "dur": dur, "lat": lat, "banks": banks,
                    "boost": boost[0]})
        return me

    def tt(out, a, b, op):
        cyc = 1 if (a["ps"] or b["ps"]) else 2
        add("dve", "c", lambda e: [e.tensor_tensor(out["a"], a["a"], b["a"], op)], [a, b], [out],
            50 + max(64, out["cnt"] * cyc) * CY)

    def ts(out, a, s1, s2, op0, op1=None):
        R = [a] + [s for s in (s1, s2) if isinstance(s, dict)]
        v1 = s1["a"] if isinstance(s1, dict) else s1
        v2 = s2["a"] if isinstance(s2, dict) else s2
        half = 0.5 if out["sz"] == 2 and a["sz"] == 2 else 1

        def emit(e):
            if op1 is None:
                return [e.tensor_scalar(out["a"], a["a"], v1, None, op0)]
            return [e.tensor_scalar(out["a"], a["a"], v1, v2, op0, op1)]
        add("dve", "c", emit, R, [out], 50 + max(64, out["cnt"] * half) * CY)

    def cp(out, a):
        add("dve", "c", lambda e: [e.tensor_copy(out["a"], a["a"])], [a], [out], 50 + max(64, out["cnt"]) * CY)

    def act(out, a, scale=1.0, bias=0.0, func=None):
        f = func if func is not None else (AF.Copy if bias == 0.0 else AF.Identity)
        add("act", "c", lambda e: [e.activation(out["a"], a["a"], f, bias=bias, scale=scale)], [a], [out],
            65 + max(64, out["cnt"]) * CY)

    def gather(eng, out, win, off, scale=1.0, bias=0.0, other=None, op=None):
        dur = 60 + out["cnt"] * GA * CY
        if eng == "act":
            f = AF.Copy if bias == 0.0 else AF.Identity
            add("act", "c", lambda e: [e.activation(out["a"], win["a"].indirect(off["a"]), f, bias=bias, scale=scale)],
                [win, off], [out], dur)
        elif other is None:
            add("dve", "c", lambda e: [e.tensor_scalar(out["a"], win["a"].indirect(off["a"]), scale, bias, A.mult, A.add)],
                [win, off], [out], dur)
        else:
            add("dve", "c", lambda e: [e.tensor_tensor(out["a"], win["a"].indirect(off["a"]), other["a"], op)],
                [win, off, other], [out], dur)
        ops[-1]["gat"] = True

    def mm(items):
        R, W, dur = [], [], 0.0
        for o, l, r, st, sp in items:
            R += [l, r] + ([] if st else [o])
            W.append(o)
            dur += (max(64, r["cnt"]) * (4 if r["sz"] == 4 else 1) + 16) * PCY
        add("pe", "c", lambda e: [e.matmul(o["a"], l["a"], r["a"], st, sp) for o, l, r, st, sp in items], R, W, dur, 60)

    def group(items, start=True):
        mm([(o, l, r, start and k == 0, k == len(items) - 1) for k, (o, l, r) in enumerate(items)])

    def iota(out, pattern, base, mult):
        kw = {} if SCRATCH[out["n"]][2] == I else {"allow_small_or_imprecise_dtypes": True}
        add("pool", "c", lambda e: [e.iota(out["a"], pattern, base, mult, **kw)], [], [out], 130 + 2 * out["cnt"] * CY)

    def dma(out, a, accum=False):
        side = out if out["n"] in SCRATCH else a
        by = side["cnt"] * side["sz"] * (side["p"][1] - side["p"][0])
        if accum:
            add("pool", "d", lambda e: [e.dma_start(out["a"], a["a"], accum_op=A.add)], [a, out], [out],
                900.0, 1800 + by / 300.0)
        else:
            add("sync", "d", lambda e: [e.dma_start(out["a"], a["a"])], [a], [out], 100.0, 1800 + by / 500.0)

    nrem = [0, 0]

    def send(pairs):
        k = nrem[0]
        nrem[0] += 1
        eng = topo.engines(core, down)
        per = len(eng) // len(pairs)
        rid, pid = topo.addr(down)[0], topo.addr(down)[1]

        def emit(e):
            tr = [RemoteDMATransfer(dst_ids=[DstId(rid=rid, pnc=pid)],
                                    dma_engine_mask=sum(1 << x for x in eng[j * per:(j + 1) * per]),
                                    remote_sem=T.sem["rr%d" % k], src=s["a"], dst=d["a"])
                  for j, (d, s) in enumerate(pairs)]
            e.remote_dma_fused(tr, local_sem=T.sem["rl%d" % loc])
        loc = nrem[1]
        nrem[1] += 1
        by = sum(s["cnt"] * s["sz"] * 128 for d, s in pairs)
        me = add("pool", "r", emit, [s for d, s in pairs], [d for d, s in pairs], 1000.0, 2500 + by / 70.0)
        ops[me].update(rem=(k, per * len(pairs)), loc=loc, eng_t=by / 140.0)

    nland = [0, 0]

    def bounce(hi_, alu, items, relay=()):
        k = nrem[0]
        nrem[0] += 1 + (len(relay) > 0)
        helper = mates[hi_]
        w = items[0][1][0]["cnt"]
        home = [x[0] for x in items if x[0] is not None]
        land = []
        for x in items:
            if nland[hi_] % 4096 + w > 4096:
                nland[hi_] += 4096 - nland[hi_] % 4096
            a = nland[hi_] % 16384
            land.append(c2(("LO0", "LO1", "HI0", "HI1")[a // 4096], a % 4096, a % 4096 + w))
            nland[hi_] += w

        def masks(eng, m):
            per = 1
            while 2 * per * m <= len(eng):
                per *= 2
            return per, [sum(1 << x for x in eng[j * per:(j + 1) * per]) for j in range(m)]

        def dst(c):
            return [DstId(rid=topo.addr(c)[0], pnc=topo.addr(c)[1])]
        pin, out = masks(topo.engines(core, helper), len(items))
        far = topo.engines(helper, down) if hi_ == 0 else []
        pbk, back = masks([e for e in topo.engines(helper, core) if e not in far], len(items))
        pfr, on = masks(far, len(relay)) if relay else (0, [])

        def emit(e):
            e.remote_dma_fused([RemoteDMATransfer(dst_ids=dst(helper), dma_engine_mask=m, remote_sem=T.sem["rr%d" % k],
                                                  srcs=[s["a"] for s in x[1]], dsts=[z["a"]], alu_op=alu if len(x[1]) > 1 else 0)
                                for m, x, z in zip(out, items, land)], local_sem=T.sem["bl" if home else "rr%d" % k])

        def hand_on(e):
            e.wait_ge(T.sem["rr%d" % k], pin * len(items))
            tr = [RemoteDMATransfer(dst_ids=dst(core), dma_engine_mask=m, remote_sem=T.sem["rr%d" % k], src=z["a"], dst=x[0]["a"])
                  for m, x, z in zip(back, items, land) if home]
            tr += [RemoteDMATransfer(dst_ids=dst(down), dma_engine_mask=m, remote_sem=T.sem["rr%d" % (k + 1)],
                                     src=land[j]["a"], dst=z["a"]) for m, (z, j) in zip(on, relay)]
            e.remote_dma_fused(tr, local_sem=T.sem["bl"])
            return pbk * len(home) + pfr * len(relay)
        srcs = [s for x in items for s in x[1]]
        mine = sum(s["cnt"] * 512 for s in srcs) / 500.0
        there = [dict(z, n="%d%s" % (hi_, z["n"])) for z in land]
        me = add("pool", "b", emit, srcs, home + there, 1000.0,
                 5000 + mine + w * 512 * len(home) / 300.0, [z for z, j in relay])
        ops[me].update(rem=(k, (pbk if home else pin) * len(items), pfr * len(relay), pin * len(home)),
                       helper=(hi_, hand_on), eng_t=mine, far=w * 512 * len(relay) / 70.0)

    def credit(regions):
        k = nrem[0]
        nrem[0] += 1
        rid, pid = topo.addr(up)[0], topo.addr(up)[1]
        m = 1 << topo.engines(core, up)[0]
        loc = nrem[1]
        nrem[1] += 1
        me = add("pool", "r", lambda e: e.remote_sem_update(T.sem["rr%d" % k], T.sem["rl%d" % loc], pid, rid, m),
                 [], regions, 800.0, 2500.0)
        ops[me].update(rem=(k, 1), loc=loc)

    def shift(name, a, w, src=None, s=None):
        src, s = (name, a) if src is None else (src, s)
        dma(c2(name, 3072 + a, 3072 + a + w, part=slice(0, 112)), c2(src, s, s + w, part=slice(16, 128)))
        dma(c2(name, 3072 + a, 3072 + a + w, part=slice(112, 128)), c2(src, s, s + w, part=slice(0, 16)))

    def publish(names, a, w):
        send([(c2(x, 2048 + a, 2048 + a + w), c2(x, a, a + w)) for x in names])
        for x in names:
            shift(x, a, w)

    p1, n1, nh, w12, w20 = [ap(x) for x in ("P1", "N1", "NH", "W12", "W20")]
    idf, idn, id4, id8 = ap("IDF"), ap("IDN"), ap("ID4"), ap("ID8")

    dma(c2("IN1", 0, 1024), c2("th", 0, 1024))
    dma(c2("IN1", 1024, 2048), c2("dl", 0, 1024))
    iota(ap("XD"), [[1, 128]], 0, -1)
    send([(c2("IN1", 4096, 6144), c2("IN1", 0, 2048))])
    dma(c2("IN1", 2048, 3072), c2("th", 1024, 2048))
    dma(c2("IN1", 3072, 4096), c2("dl", 1024, 2048))
    dma(ap("SLI"), ap("sl"))
    dma(ap("RFI"), ap("rf"))
    dma(ap("LE0"), ap("dr"))
    for w, x in ((p1, 1.0), (n1, -1.0), (nh, -0.5), (w12, -4096.0), (w20, 2.0 ** 20), (idf, 1.0), (idn, -1.0), (id4, 4.0), (id8, 8.0)):
        ts(w, ap("XD"), 0.0, x, A.is_equal, A.mult)
    iota(c2("PC", 0, 1), [[0, 1]], 0, 1)
    iota(ap("XI"), [[1, 144]], -16, 0)
    iota(ap("VI"), [[0, 4], [1024, 2], [16, 32]], 0, 0)
    iota(ap("CJ"), [[0, 2], [-4096, 4], [0, 16]], 16384, 0)
    ts(c2("PC", 1, 2), c2("PC", 0, 1), 112, None, A.bitwise_and)
    ts(c2("PC", 2, 3), c2("PC", 0, 1), 15, None, A.bitwise_and)
    ts(c2("PC", 3, 4), c2("PC", 2, 3), 1, None, A.arith_shift_right)
    ts(c2("PC", 4, 5), c2("PC", 0, 1), 4, 1, A.arith_shift_right, A.bitwise_and)
    cp(c2("PF", 0, 5), c2("PC", 0, 5))
    g16, pm, ph = c2("PF", 1, 2), c2("PF", 2, 3), c2("PF", 3, 4)
    ts(c2("PF", 16, 18), c2("XI", 16, 18), c2("PF", 4, 5), None, A.is_equal)
    for s in range(2):
        for e in range(2):
            ts(c2("WS", 128 * (2 * s + e), 128 * (2 * s + e) + 128), ap("XD"), 16.0 * (e - s), c2("PF", 16 + s, 17 + s),
               A.is_equal, A.mult)
    add("dve", "c", lambda e: [e.memset(T["XT"][:], 0.0)], [], [ap("XT")], 50 + 512 * CY)
    ts(c2("PF", 8, 16), c2("XI", 16, 24), ph, None, A.is_equal)
    ts(c2("UP", 0, 144), ap("XI"), g16, 16384.0, A.is_equal, A.mult)
    ts(c2("UP", 144, 288), ap("XI"), g16, 32768.0, A.is_equal, A.mult)
    ts(c2("UN", 0, 144), ap("XI"), g16, -32768.0, A.is_equal, A.mult)
    ts(c2("UN", 144, 288), ap("XI"), g16, -16384.0, A.is_equal, A.mult)
    for j in range(5):
        ts(c2("YM", 144 * j, 144 * j + 144), ap("XI"), g16, c2("PF", 8 + j, 9 + j), A.is_equal, A.mult)
    ts(ap("VC0"), ap("VI"), pm, -MID, A.add, A.add)
    ts(ap("VC1"), ap("VC0"), 512.0, None, A.add)
    ts(c2("CM", 0, 256), ap("VI"), 0.0, 1.0 / 128, A.mult, A.add)
    ts(c2("PF", 19, 20), c2("PF", 12, 13), -1.0, 1.0, A.mult, A.add)
    for par in range(2):
        for kk in range(2):
            cp(ap("SP%d" % par, al, al, kk), ap("SLI", al, par + 2 * kk))
        cp(ap("SU%d" % par), ap("SP%d" % par))
    ts(ap("RR"), ap("RFI"), -MID, None, A.add)

    bank = [("KA", 0), ("KA", 512), ("KA", 1024), ("KB", 0), ("KB", 512), ("KB", 1024)]
    nb = [0]

    def ends(src, dst0):
        for a in (0, 512):
            for tab, sg in (("LO0", n1), ("HI0", p1)):
                bn, bo = bank[nb[0] % 6]
                nb[0] += 1
                ps = c2(bn, bo, bo + 512)
                group([(ps, p1, c2("IN1", src + a, src + a + 512)), (ps, sg, c2("IN1", src + 1024 + a, src + 1536 + a))])
                if tab == "LO0":
                    act(c2(tab, dst0 + a, dst0 + a + 512), ps, scale=-0.0625, bias=-5.0 / 256)
                else:
                    ts(c2(tab, dst0 + a, dst0 + a + 512), ps, 0.0625, 3.0 / 256, A.mult, A.add)
    ends(0, 0)
    shift("LO0", 0, 1024)
    shift("HI0", 0, 1024)
    ends(2048, 1024)
    ends(4096, 2048)
    send([(c2("LE1", 0, 1024), c2("LE0", 0, 1024))])

    def steps(a):
        dr = c2("LE%d" % (a // 2048), a % 2048, a % 2048 + 1024)
        act(c2("FS", a, a + 1024), dr, scale=0.0625)
        act(c2("FM", a, a + 1024), dr, scale=-0.0625, bias=1.0 / 128)
    steps(0)
    steps(1024)

    def tables(par):
        srcs = [ap("SP%d" % par, al, j) for j in range(4)] + [ap("RR", al, al, par)]
        for j, x in enumerate(srcs):
            dh, dl = ap("XT", al, al, slice(2 * j, 32, 16)), ap("XT", al, al, slice(2 * j + 1, 32, 16))
            act(dh, x)
            tt(dl, x, dh, A.subtract)
        xu = "XU%d" % par
        add("dve", "c", lambda e: [e.transpose(T[xu][:], T["XT"][:])], [ap("XT")], [ap(xu)], 50 + 512 * CY)

    def tables_out(par):
        a, xu = 512 * par, "XU%d" % par
        for kk in range(2):
            mm([(ap("PI", al, al, slice(16 * s, 16 * s + 16)), c2("WS", 128 * (2 * s + e), 128 * (2 * s + e) + 128),
                 ap(xu, al, slice(16 * kk, 16 * kk + 16), slice(16 * e, 16 * e + 16)), e == 0, e == 1)
                for s in range(2) for e in range(2)])
            act(c2("ST", a + 1024 * kk, a + 1024 * kk + 512), ap("PI"))
            if kk == 0:
                publish(["ST"], a, 512)
        if par == 0:
            stop = c2("ST", 2048, 2049)
            ts(stop, stop, c2("PF", 19, 20), c2("PF", 12, 13), A.mult, A.add)

    def pick(out, j, w, g0):
        return [(out, c2("YM", 144 * j + 16 - r, 144 * j + 144 - r), c2("GB", g0 + r, g0 + 16 * w, 16)) for r in range(16)]

    def fetch(t, kk):
        par = t % 2
        lo, hi = "LO%d" % par, "HI%d" % par
        a = 512 * (par + 2 * kk)
        dma(ap("GH%d" % kk, al, al, 4), c2(hi, a, a + 512))
        for h in range(2):
            for m in range(2):
                for j in range(4):
                    o = 64 * j + 32 * kk + 16 * h
                    mine = kk == 0 and h == 0 and (j >= 4 - OPT["vg0"] // 2 if t == 0 else m == 1 and j >= 4 - OPT["vg"])
                    eng = "dve" if mine else "act"
                    if m == 1:
                        gather(eng, ap("GH%d" % kk, al, h, j), ap(hi), c2("SU%d" % par, o, o + 16))
                    elif kk == 0 or h == 0:
                        w = 16 + 16 * kk
                        gather(eng, ap("GL%d" % kk, al, j, slice(256 * h, 256 * h + 16 * w)), ap(lo),
                               c2("SU%d" % par, o, o + w), scale=-1.0, bias=-1.0 / 128)

    def chunk(t, k):
        par = t % 2
        kk, h = k // 2, k % 2
        c = 4 * t + k
        lo, nlo, nhi = "LO%d" % par, "LO%d" % (1 - par), "HI%d" % (1 - par)
        gl, gh, ind, ks = "GL%d" % kk, "GH%d" % kk, "IN1", "KB"
        rb, lt = ap("RB%d" % (c % 2)), "LT%d" % kk
        v0 = 512 * (par + 2 * kk) + 256 * h

        def key(i, w=1):
            return c2(ks, 256 * i, 256 * (i + w))

        def src(name, i, w=1):
            if name[:2] in ("GH", "LT", "LE"):
                return ap(name, al, h, slice(i, i + w))
            return ap(name, al, slice(i, i + w), slice(256 * h, 256 * h + 256))

        def bit(s, i, w=1):
            o = 1280 * (s + 2 if s > 1 else s + 2 * (c % 2)) + 256 * i
            return c2(ind, o, o + 256 * w)

        def low_(i, w=1):
            return c2("KA", 256 * i, 256 * (i + w))

        for i in (0, 2):
            if k in OPT["pelo"]:
                group([(low_(i, 2), idf, src(gl, i, 2))])
            else:
                act(low_(i, 2), src(gl, i, 2))
        own = c2(lo, v0, v0 + 256)
        act(low_(4), own, scale=-1.0, bias=-1.0 / 128)
        tt(bit(0, 1, 4), low_(1, 4), src(gl, 0, 4), A.is_ge)
        tt(bit(0, 0), low_(4), src(gl, 0), A.is_lt)
        tt(bit(1, 2, 3), low_(2, 3), src(gl, 0, 3), A.is_ge)
        tt(bit(1, 0, 2), low_(3, 2), src(gl, 0, 2), A.is_lt)
        for a, b in OPT["cuts"][k]:
            for rot in range(1, 5):
                for x, y in ((a, min(b, 5 - rot)), (max(a, 5 - rot), b)):
                    if y > x:
                        tt(bit(1 + rot, x, y - x), low_(x, y - x), src(gh, (x + rot) % 5, y - x), A.is_gt)
        back = {0: [(0, 2, 0, 1), (0, 2, 1, 2)], 2: [(2, 2, 0, 3), (2, 1, 1, 4), (3, 1, 1, 0)], 4: [(4, 1, 0, 0), (4, 1, 1, 1)]}
        for i, w in ((0, 2), (2, 2), (4, 1)):
            parts = [[(key(i, w), idf, src(gl, i, w)) if i < 4 else (key(4), idn, own)],
                     [(key(i, w), p1, bit(s, i, w)) for s in range(2)] + [(key(x, ww), n1, bit(s, y, ww)) for x, ww, s, y in back[i]],
                     [(key(i, w), n1, bit(s, i, w)) for s in range(2, 4)], [(key(i, w), n1, bit(s, i, w)) for s in range(4, 6)]]
            if i == 4:
                group([x for p in parts for x in p] + [(key(4), n1, c2("CM", 0, 256))])
            else:
                for m, p in enumerate(parts):
                    mm([(o, l, r, m == 0, m == 3 and x == 1) for x, (o, l, r) in enumerate(p)])
        kcn = "KC%d" % (c % 2)
        kc, kd = c2(kcn, 0, 256), c2(kcn, 256, 512)

        def chain(out, op):
            if OPT["wide"]:
                act(ap(kcn), key(0, 2))
                tt(ap(kcn), key(2, 2), ap(kcn), op)
                tt(key(5), key(4), kc, op)
                tt(out, key(5), kd, op)
            else:
                act(kc, key(0))
                for j in range(1, 4):
                    tt(kc, key(j), kc, op)
                tt(out, key(4), kc, op)
        top = key(5)
        boost[0] = OPT["end"] if c == 15 else OPT["edge"] if k == 3 else 0.0
        chain(top, A.max)
        if k in OPT["vround"]:
            ts(rb, top, RND1, -RND1, A.add, A.add)
        else:
            act(rb, top, bias=RND1)
            act(rb, rb, bias=-RND1)
        newlo, newhi = c2(nlo, v0, v0 + 256), c2(nhi, v0, v0 + 256)
        low, na = c2("AS", 256 * h, 256 * h + 256), c2("NA%d" % kk, 256 * h, 256 * h + 256)
        if kind(t, k) == "P":
            for i in (0, 2):
                mm([(key(i, 2), idf, src(gh, i, 2), True, False)])
        tt(top, top, rb, A.subtract)
        if t < 3:
            act(newlo, top, scale=-1.0)
        else:
            act(low, top)
            act(na, low, scale=-1.0, bias=1.0 / 128)
        if kind(t, k) == "D":
            act(na, newlo, bias=1.0)
            for j in range(5):
                dma(c2("N5", 256 * j, 256 * j + 256), na)
            dma(src(gh, 0, 5), ap("N5"), accum=True)
            for x, y in ((0, 3), (3, 2)):
                act(src(lt, x, y), src(gh, x, y), scale=-1.0, bias=1.0 - 2.0 ** -21, func=AF.Sign)
        for j in range(0 if kind(t, k) == "D" else 5):
            tt(src(lt, j), top, src(gh, j), A.is_gt)
        keep, boost[0] = boost[0], 0.0
        if (t, k) in OPT["vle"]:
            for j in range(4):
                tt(src("LE%d" % kk, j), top, src(gl, j), A.is_ge)
        if kind(t, k) == "P":
            boost[0] = keep
            for i in (0, 2):
                mm([(key(i, 2), p1, src(lt, i, 2), False, True)])
            group([(key(4), idf, src(gh, 4)), (key(4), p1, src(lt, 4))])
            mn = newhi if t < 3 else low_(5)
            chain(mn, A.min)
            if t == 3:
                tt(newlo, mn, low, A.add)
                tt(newhi, mn, na, A.add)
            boost[0] = 0.0
            return
        dma(src(gh, 0, 5), src(lt, 0, 5), accum=True)
        if kind(t, k) == "F":
            waiting.append((newlo, newhi, low, na, ap("OL%d" % h), [ap(gh, al, h, j) for j in range(5)],
                            [c2(x, 2048 + v0, 2304 + v0) for x in (nlo, nhi)]))
            if OPT["pair"] and k == 0:
                return
            far = range(len(waiting) if kk == 0 else 0)
            if t < 3:
                bounce(0, 3, [(x[1], x[5]) for x in waiting], [(waiting[m][6][1], m) for m in far])
            else:
                bounce(0, 3, [(x[4], x[5]) for x in waiting])
                bounce(0, 1, [(x[e], [x[4], x[2 + e]]) for x in waiting for e in range(2)],
                       [(waiting[m][6][e], 2 * m + e) for m in far for e in range(2)])
            del waiting[:]
            return
        top = low_(5)
        act(top, src(gh, 0))
        for j in range(1, 4):
            tt(top, top, src(gh, j), A.min)
        if kind(t, k) == "D":
            tt(top, top, src(gh, 4), A.min)
            tt(newhi, top, newlo, A.subtract)
        elif t < 3:
            tt(newhi, top, src(gh, 4), A.min)
        else:
            tt(top, top, src(gh, 4), A.min)
            tt(newlo, top, low, A.add)
            tt(newhi, top, na, A.add)

    waiting = []

    def kind(t, k):
        return OPT["kinds"][t][k]

    def holds(t, kk):
        par = t % 2
        gl, le, lt = "GL%d" % kk, "LE%d" % kk, "LT%d" % kk
        byv = [(t, 2 * kk + h) in OPT["vle"] for h in range(2)]
        sgn = [kind(t, 2 * kk + h) == "D" for h in range(2)]
        halves = ((0, 2),) if byv[0] == byv[1] and sgn[0] == sgn[1] else ((0, 1), (1, 1))
        for h0, hn in ((0, 2),) if byv[0] == byv[1] else halves:
            q = slice(256 * h0, 256 * (h0 + hn))
            a = 512 * (par + 2 * kk) + 256 * h0
            na = c2("LO%d" % (1 - par), a, a + 256 * hn) if t < 3 else ap("NA%d" % kk, al, q)
            m = OPT["many"]
            for j in range(0 if byv[h0] or m == 1 else m):
                dma(ap("N4", al, j, q), na)
            for j in range(0 if byv[h0] else 4):
                if j % m == 0:
                    dma(ap(gl, al, slice(j, j + m), q), na if m == 1 else ap("N4", al, slice(0, m), q), accum=True)
                act(ap(le, al, slice(h0, h0 + hn), j), ap(gl, al, j, q), scale=-1.0,
                    bias=2.0 ** -21 + (1.0 / 128 if t == 3 else 0.0), func=AF.Sign)
        for h0, hn in halves:
            o = c2("PL", 128 * kk + 64 * h0, 128 * kk + 64 * (h0 + hn))
            part = [(c2("PL", 128 * kk + 64 * h, 128 * kk + 64 * h + 64), slice(16 * h, 16 * h + 16)) for h in range(h0, h0 + hn)]
            un, up_ = 144 * sgn[h0], 144 * byv[h0]
            bias = -294912.0 - 262144.0 * sgn[h0] + 262144.0 * (not byv[h0])

            def col(name, r):
                return ap(name, al, slice(h0, h0 + hn), slice(0, 4), slice(r, 256, 16))
            group([(o, c2("UN", un + 16 - r, un + 144 - r), col(lt, r)) for r in range(16)]
                  + [(o, p1, c2("CJ", 0, 64 * hn))] + [(x, idf, ap("SP%d" % par, al, al, kk, q)) for x, q in part]
                  + [(o, c2("UP", up_ + 16 - r, up_ + 144 - r), col(le, r)) for r in range(16)])
            for x, q in part:
                act(ap("KS%d" % par, al, al, kk, q), x, bias=bias - MID)
        if t == 3:
            elect(3, slice(kk, kk + 1), slice(0, 32))

    def drift(t):
        par = t % 2
        lo, hi, nlo, nhi = "LO%d" % par, "HI%d" % par, "LO%d" % (1 - par), "HI%d" % (1 - par)
        if t < 3:
            items = [(c2(new, a, a + 512), [c2(old, a, a + 512), c2(step, a, a + 512)])
                     for a in range(512 * (1 - par), 3072, 1024) for new, old, step in ((nlo, lo, "FM"), (nhi, hi, "FS"))]
            for new, (old, step) in items[:OPT["here"]]:
                dma(new, old)
                dma(new, step, accum=True)
            if items[OPT["here"]:]:
                bounce(1, 1, items[OPT["here"]:])
            for new in (nlo, nhi):
                shift(new, 512 * (1 - par), 512)
        elif OPT["here"] == 6:
            for a in (0, 1024):
                act(c2(nlo, a, a + 512), c2(lo, a, a + 512), scale=-1.0, bias=-1.0 / 128)
                act(c2(nhi, a, a + 512), c2(lo, a, a + 512), bias=1.0 / 64)
                for new, x in ((nhi, hi), (nlo, hi), (nlo, "FS"), (nlo, "FS")):
                    dma(c2(new, a, a + 512), c2(x, a, a + 512), accum=True)
            publish([nlo, nhi], 0, 512)
        else:
            items = []
            for a in (0, 1024):
                pos, neg = ap("YB%d" % (a // 1024)), c2("FM", a + 512, a + 1024)
                act(pos, c2(lo, a, a + 512), scale=-1.0, bias=-1.0 / 128)
                act(neg, c2(lo, a, a + 512), bias=1.0 / 64)
                items += [(c2(nlo, a, a + 512), [pos] + [c2(x, a, a + 512) for x in (hi, "FS", "FS")]),
                          (c2(nhi, a, a + 512), [neg, c2(hi, a, a + 512)])]
            bounce(0, 1, items, [(c2(nlo, 2048, 2560), 0), (c2(nhi, 2048, 2560), 1)])
            for new in (nlo, nhi):
                shift(new, 0, 512)

    def elect(t, q, cq):
        par = t % 2
        spn, ksn = "SP%d" % par, "KS%d" % par
        w = (q.stop - q.start) * (cq.stop - cq.start)
        boost[0] = OPT["boost"] * (OPT["last"] if t >= 2 else 1)

        def cut(name, i, m=1, base=0):
            base += q.start * {"SB": 160, "M2": 64}.get(name, 128)
            return c2(name, base + w * i, base + w * (i + m))
        kt, d = [cut("SM", i) for i in range(2)]
        take, o1, o2, top, ktp = [cut("SB", i) for i in range(5)]
        tj = cut("TJ", 0, 4)
        ix = [c2("IX", 64 * i + 32 * q.start, 64 * i + 32 * q.start + w) for i in range(4)]
        g0 = 512 * q.start
        rr, rows, ks = ap("RR", al, q, par, cq), ap(spn, al, al, q, cq), ap(ksn, al, al, q, cq)
        gb, stay, nv, thr, ch = c2("GB", g0, g0 + 16 * w), cut("STAY", 0, 4), cut("NV", 0, 4), cut("THR", 0, 4), cut("CH", 0, 4)
        tt(cut("M2", 0, 2), ap(ksn, al, slice(0, 2), q, cq), ap(ksn, al, slice(2, 4), q, cq), A.max)
        tt(kt, cut("M2", 0), cut("M2", 1), A.max)
        ts(top, kt, RND12, -RND12, A.add, A.add)
        tt(cut("PL", 0, 1, 256), kt, top, A.subtract)
        act(stay, ks, func=AF.Sign)
        act(ktp, top, func=AF.Relu)
        act(ch, ks, bias=RND12)
        act(tj, ch, bias=-RND12)
        for m in range(3):
            ts(ix[m], cut("PL", m, 1, 256), MID, 2048.0, A.add, A.min)
            if m == 0:
                tt(d, cut("PL", 0, 1, 256), rr, A.subtract)
            gather("act", gb, c2("ST", 0, 2049), ix[m])
            group(pick(cut("PL", m + 1, 1, 256), 4, w, g0))
        tt(cut("EQ", 0, 4), cut("PL", 0, 4, 256), ap("VC%d" % par, al, al, q, cq), A.is_equal)
        group([(cut("PI", 0), w20, cut("EQ", m)) for m in range(4)])
        tt(take, cut("PI", 0), kt, A.is_lt)
        tt(d, d, take, A.mult)
        tt(rr, rr, d, A.add)
        ts(ix[3], rr, MID, None, A.add)
        gather("act", gb, ap("ST"), ix[3])
        if t < 3:
            credit([c2("ST", 2048 + 512 * par, 2560 + 512 * par)])
        ts(o1, rr, 0.0, 2048.0, A.is_gt, A.mult)
        ts(o2, rr, 1024.0, 1024.0, A.is_gt, A.mult)
        group([(cut("PI", 0, 4, 256), n1, tj)] + [(cut("PI", j, 1, 256), l, r) for j in range(4) for l, r in ((p1, ktp), (w20, take))])
        act(nv, cut("PI", 0, 4, 256), bias=-0.25, func=AF.Sign)
        group([(cut("PI", 0, 4), w12, stay), (cut("PI", 0, 4), w12, nv)]
              + [(cut("PI", j), l, r) for j in range(4) for l, r in ((nh, o1), (p1, o2))])
        act(thr, cut("PI", 0, 4), bias=4096.0)
        y = cut("PL", 0, 4, 256)
        for j in range(4):
            o = cut("PL", j, 1, 256)
            group([(o, p1, o1), (o, p1, o2)] + pick(o, j, w, g0))
        tt(ch, y, thr, A.is_lt)
        tt(y, y, rows, A.subtract)
        tt(y, y, ch, A.mult)
        tt(rows, y, rows, A.add)
        if w == 64:
            cp(ap("SU%d" % par), rows)
        else:
            for j in range(4):
                o = 64 * j + 32 * q.start + cq.start
                cp(c2("SU%d" % par, o, o + w), ap(spn, al, j, q.start, cq))
        if t < 3:
            tables(par)
            tables_out(par)
        boost[0] = 0.0

    for par in range(2):
        tables(par)
    for t in range(4):
        par = t % 2
        for kk in range(2):
            fetch(t, kk)
            if kk == 0:
                if t == 0:
                    gate[0] = len(ops) - 1
                    steps(2048)
                    for x in range(2):
                        tables_out(x)
                    gate[0] = None
                boost[0] = OPT["early"]
                drift(t)
                boost[0] = 0.0
            chunk(t, 2 * kk)
            chunk(t, 2 * kk + 1)
            if kk == 0:
                for x in ("LO%d" % (1 - par), "HI%d" % (1 - par)):
                    shift(x, 512 * par, 512)
                    todo = [h for h in range(2) if kind(t, h) != "F" or (t < 3 and x[0] == "L")]
                    if todo:
                        a, b = 512 * par + 256 * todo[0], 512 * par + 256 * todo[-1] + 256
                        if x[0] in OPT["relay"]:
                            bounce(0, 0, [(None, [c2(x, a, b)])], [(c2(x, 2048 + a, 2048 + b), 0)])
                        else:
                            send([(c2(x, 2048 + a, 2048 + b), c2(x, a, b))])
            holds(t, kk)
        if t < 3:
            a, b = (2048, 3072) if t == 2 else (2560 - 512 * par, 3072 - 512 * par)
            credit([c2("LO%d" % par, a, b), c2("HI%d" % par, a, b)])
            elect(t, slice(0, 2), slice(0, 32))

    for a in range(4):
        act(c2("FM", 512 * a, 512 * a + 512), c2("LO0", 512 * a, 512 * a + 512), scale=8.0)
        dma(c2("yt", 512 * a, 512 * a + 512), c2("FM", 512 * a, 512 * a + 512))
    add("pe", "c", lambda e: [e.transpose(T["PI"][:, 0:4], T["RR"][:], T["IDF"][:])], [ap("RR"), idf],
        [c2("PI", 0, 128)], 300.0, 60)
    act(ap("RFT"), c2("PI", 0, 128), bias=MID)
    for gi in range(8):
        dma(ap("yr", gi), c2("RFT", 16 * gi, 16 * gi + 16))
    for s, (a, x, w) in enumerate(((0, 0, 512), (2, 0, 512), (1, 0, 512), (3, 0, 256), (3, 256, 256))):
        par, kk, zo, v0 = a % 2, a // 2, 2048 * (s % 2), 512 * a + x
        own = c2("GL0", v0, v0 + w)
        dma(own, c2("LO0", v0, v0 + w))
        ps = c2("KA" if s % 2 == 0 else "KB", 512 * (s // 2), 512 * (s // 2) + w)
        yb = c2("YB%d" % (s % 2), 0, w)
        fold = s in OPT["fsum"]
        terms = [c2("GL1", v0, v0 + w)]
        if fold:
            act(terms[0], c2("HI0", v0, v0 + w), scale=0.5)
        else:
            mm([(ps, id4, c2("HI0", v0, v0 + w), True, False)])
        for j in range(4):
            o = 64 * j + 32 * kk + x // 16
            off = c2("SU%d" % par, o, o + w // 16)
            z = c2("LO1", zo + 512 * j, zo + 512 * j + w)
            p = c2("HI1", zo + 512 * j, zo + 512 * j + w)
            if j >= OPT["fin"][s]:
                gather("act", z, ap("LO0"), off, scale=-1.0)
                dma(z, own, accum=True)
                act(z, z, scale=-8.0, func=AF.Sigmoid)
            else:
                gather("dve", z, ap("LO0"), off, other=own, op=A.subtract)
                act(z, z, scale=8.0, func=AF.Sigmoid)
            if s == 0 and j == 0 and not lite:
                ops[-1]["dur"] += 1300.0
                first = len(ops) - 1
            elif not lite:
                ops[-1]["deps"].add((first, "R"))
            gather("dve", p, ap("HI0"), off, other=z, op=A.mult)
            terms.append(p)
            if not fold:
                mm([(ps, id8, p, False, j == 3)])
        if fold:
            bounce(1, 1, [(yb, terms)])
            act(yb, yb, scale=8.0)
        else:
            act(yb, ps)
        dma(c2("yq", v0, v0 + w), yb)
    return ops


def schedule(ops):
    n = len(ops)
    eng = [o["eng"] for o in ops]
    banks = [sorted(o["banks"]) for o in ops]
    pred = [sorted(set((d, w == "X") for d, w in o["deps"])) for o in ops]
    succ = [[] for _ in range(n)]
    for i in range(n):
        for d, x in pred[i]:
            succ[d].append((i, x))

    def costs(ds, rs, ls, cs, ss, ps, gs, hop):
        dur, lat, use, far = [], [], [], []
        for o in ops:
            d, l, u = o["dur"], o["lat"], o.get("eng_t")
            if o["kind"] == "d":
                d, u = d * ds, (l - 1800) * ds
                l = 1800 * (1 + ds) / 2 + u
            elif o["kind"] == "b":
                d, l, u = d * rs, l * rs, u * ds
            elif o["kind"] == "r":
                d, l, u = d * rs, 2500 * rs + (l - 2500) * ls, u and u * ls
            else:
                d *= {"dve": cs, "pe": ps, "act": ss}.get(o["eng"], 1) * (gs if o.get("gat") else 1)
            dur.append(d)
            lat.append(l)
            use.append(u)
            far.append(o.get("far", 0.0) * ls)
        return dur, lat, use, far, hop

    def sweep(cost, prio, back, look, beta):
        dur, lat, use, far, hop = cost
        before, after = (succ, pred) if back else (pred, succ)
        left = [len(p) for p in before]
        free, bfree, blast, dfree = {e: 0.0 for e in eng}, {}, {}, 0.0
        done = [0.0] * n
        rdy = list(lat) if back else [0.0] * n
        ready = set(i for i in range(n) if left[i] == 0)
        order, extra = [], []
        while ready:
            est = {}
            for i in ready:
                s = max(rdy[i], free[eng[i]])
                for b in banks[i]:
                    if b in blast and eng[blast[b]] != eng[i] and bfree[b] + hop > s:
                        s = bfree[b] + hop
                est[i] = s
            first = min(ready, key=lambda i: (est[i], -prio[i], i))
            e, t0 = eng[first], est[first]
            i = max((x for x in ready if eng[x] == e and est[x] <= t0 + look),
                    key=lambda x: (prio[x] - beta * (est[x] - t0), -x))
            free[e] = est[i] + dur[i]
            done[i] = free[e] + (0.0 if back else lat[i])
            if use[i] and not back:
                late = max(0.0, dfree - free[e] - 1800)
                done[i] += late
                dfree = free[e] + 1800 + late + use[i]
            for b in banks[i]:
                if b in blast and eng[blast[b]] != e:
                    extra.append((i, blast[b]))
                blast[b] = i
                bfree[b] = done[i]
            ready.discard(i)
            order.append(i)
            for s, x in after[i]:
                rdy[s] = max(rdy[s], done[i] + hop + (lat[s] if back else 0.0) + (far[s if back else i] if x else 0.0))
                left[s] -= 1
                if left[s] == 0:
                    ready.add(s)
        return order, done, extra

    def replay(cost, order, extra):
        dur, lat, use, far, hop = cost
        more = {}
        for i, d in extra:
            more.setdefault(i, []).append((d, False))
        free, dfree, done = {e: 0.0 for e in eng}, 0.0, [0.0] * n
        last, why, dlast = {}, [None] * n, None
        for i in order:
            s, why[i] = free[eng[i]], last.get(eng[i])
            for d, x in pred[i] + more.get(i, []):
                r = done[d] + hop + (far[d] if x else 0.0)
                if r > s:
                    s, why[i] = r, d
            free[eng[i]] = s + dur[i]
            last[eng[i]] = i
            done[i] = s + dur[i] + lat[i]
            if use[i]:
                late = max(0.0, dfree - s - dur[i] - 1800)
                if late > 0:
                    why[i] = dlast
                done[i] += late
                dfree, dlast = s + dur[i] + 1800 + late + use[i], i
        i, path = max(range(n), key=lambda x: done[x]), []
        while i is not None:
            path.append(i)
            i = why[i]
        return max(done), path

    tests = [costs(*x) for x in SPEEDS]
    best = None
    for plan, look, beta, cp in OPT["tries"]:
        cost = costs(*plan)
        prio = [0.0] * n
        for i in range(n - 1, -1, -1):
            prio[i] = cost[0][i] + cost[1][i] + max([prio[s] + cost[4] for s, x in succ[i]] + [0.0])
        prio = [cp * p - (1 - cp) * prio[0] * i / n + ops[i]["boost"] for i, p in enumerate(prio)]
        for turn in range(OPT["turns"]):
            order, done, extra = sweep(cost, prio, False, look, beta)
            spans = [replay(c, order, extra)[0] for c in tests]
            score = sum(WEIGHTS[k] * x / (best[1] if best else spans)[k] for k, x in enumerate(spans))
            if best is None or score < best[0]:
                best = (score, best[1] if best else spans, order, done, extra, spans, (plan, look, beta, cp, turn), prio)
            late = sweep(cost, done, True, look, beta)[1]
            prio = [OPT["mix"] * (a + OPT["keep"] * o["boost"]) + (1 - OPT["mix"]) * b for a, b, o in zip(late, prio, ops)]
    plan, look, beta = best[6][:3]
    cost, prio = costs(*plan), list(best[7])
    order, extra = best[2], best[4]
    for turn in range(OPT["mend"]):
        path = replay(tests[turn % len(tests)], order, extra)[1]
        for i, d in zip(path, path[1:]):
            if (d, False) not in pred[i] and (d, True) not in pred[i]:
                prio[i] += OPT["step"]
                prio[d] -= OPT["step"]
            else:
                prio[d] = max(prio[d], prio[i])
        order, done, extra = sweep(cost, prio, False, look, beta)
        spans = [replay(c, order, extra)[0] for c in tests]
        score = sum(WEIGHTS[k] * x / best[1][k] for k, x in enumerate(spans))
        if score < best[0]:
            best = (score, best[1], order, done, extra, spans, (plan, look, beta, "mend", turn), list(prio))
        elif turn % OPT["back"] == 0:
            prio, order, extra = list(best[7]), best[2], best[4]
    LAST["best"] = best[5:7]
    return best[2], None, best[3], best[4]


def rank_program(g, core, T, topo):
    served = [(c, k) for c in T.cores for k, h in enumerate(neighbours(c, T, topo)) if h == core]
    if T.rank_of(core) is None and not served:
        return
    key = repr(sorted(OPT.items()))
    ops = build(served[0][0] if served else core, T, topo, bool(served) and key in LAST)
    if key not in LAST:
        LAST[key] = schedule(ops)
    order, start, done, extra = LAST[key]
    if served:
        sent = sum(ops[i]["helper"][1](g) for i in order if ops[i].get("helper", (None,))[0] == served[0][1])
        if sent:
            g.wait_ge(T.sem["bl"], sent)
        return
    for i, d in extra:
        ops[i]["deps"].add((d, "W"))
    LAST["plan"] = (ops, order, start, done)
    queue = {"pe": g.tensor, "dve": g.vector, "act": g.scalar, "pool": g, "sync": g.sync}
    known = {q: {} for q in queue}
    total, waited, when = {}, {}, {}
    pools = {"pool": [["dg%d" % k, None] for k in range(NG)], "sync": [["ds%d" % k, None] for k in range(NS)]}

    def wait(q, tok):
        sem, cnt, snap = tok
        if known[q].get(sem, 0) >= cnt:
            return False
        queue[q].wait_ge(T.sem[sem], cnt)
        waited[sem] = max(waited.get(sem, 0), cnt)
        known[q][sem] = cnt
        for s, v in snap.items():
            if known[q].get(s, 0) < v:
                known[q][s] = v
        return True

    def need(q, d, w, i):
        tok = ops[d]["tok" + w]
        if known[q].get(tok[0], 0) >= tok[1]:
            return
        if ops[d].get("reused"):
            need(q, ops[d]["waiters"][0], "R", i)
        elif wait(q, tok) and ops[d]["kind"] == "d":
            ops[d]["waiters"].append(i)

    for i in order:
        o = ops[i]
        q = o["eng"]
        for d, w in sorted(o["deps"], key=lambda x: (-done[x[0]], x)):
            need(q, d, w, i)
        if o["kind"] == "c":
            sem = "e_" + q
            o["emit"](queue[q])[-1].then_inc(T.sem[sem], 1)
            total[sem] = total.get(sem, 0) + 1
            o["tokR"] = o["tokW"] = (sem, total[sem], dict(known[q]))
        elif o["kind"] == "d":
            slot = [s for s in pools[q] if s[1] is None or [w for w in ops[s[1]]["waiters"] if w != i]][0]
            if slot[1] is not None:
                for w in list(ops[slot[1]]["waiters"]):
                    if ops[w]["eng"] != q:
                        need(q, w, "R", i)
                ops[slot[1]]["reused"] = True
            pools[q].remove(slot)
            pools[q].append(slot)
            slot[1] = i
            sem = slot[0]
            o["waiters"] = []
            o["emit"](queue[q])[0].then_inc(T.sem[sem], 16)
            total[sem] = total.get(sem, 0) + 16
            o["tokR"] = o["tokW"] = (sem, total[sem], dict(known[q]))
        elif o["kind"] == "b":
            k, cnt, far, sent = o["rem"]
            o["emit"](queue[q])
            sem = "rr%d" % k
            total[sem] = cnt
            total["bl"] = total.get("bl", 0) + sent
            when["bl"] = done[i]
            o["tokR"] = o["tokW"] = (sem, cnt, dict(known[q]))
            if far:
                total["rr%d" % (k + 1)] = far
                when["rr%d" % (k + 1)] = done[i]
                o["tokX"] = ("rr%d" % (k + 1), far, {})
        else:
            k, cnt = o["rem"]
            o["emit"](queue[q])
            sem = "rl%d" % o["loc"]
            total[sem] = total["rr%d" % k] = cnt
            when["rr%d" % k] = done[i]
            o["tokR"] = (sem, cnt, dict(known[q]))
            o["tokW"] = ("rr%d" % k, cnt, {})
        when[sem] = done[i]
    for sem in sorted(total, key=lambda s: when[s]):
        if waited.get(sem, 0) < total[sem]:
            g.wait_ge(T.sem[sem], total[sem])
